import numpy as np
import ml_dtypes


def mxq(x, axis, fmt="e4m3"):
    dtype, down = {"e4m3": (ml_dtypes.float8_e4m3fn, 7), "e5m2": (ml_dtypes.float8_e5m2, 14)}[fmt]
    v = np.moveaxis(np.asarray(x, np.float32).astype(ml_dtypes.bfloat16).astype(np.float64), axis, -1)
    blocks = v.reshape(v.shape[:-1] + (-1, 32))
    amax = np.abs(blocks).max(-1, keepdims=True)
    byte = np.maximum(np.where(amax > 0, np.frexp(amax)[1] - 1 + 127, 0) - down, 1)
    scale = np.exp2(byte - 127.0)
    codes = (blocks / scale).astype(np.float32).astype(dtype).astype(np.float64)
    return np.moveaxis((codes * scale).reshape(v.shape), -1, axis)


WIDE = False


def mx_kscale(k):
    if not WIDE:
        return np.ones(k)
    levels = np.array([24, -24, 12, -12, 0])
    if k % 512:
        return np.exp2(np.random.permutation(np.resize(levels, k // 32))).repeat(32)
    a = np.empty((k // 512, 16))
    for p in range(k // 512):
        a[p, :8] = np.random.permutation(np.resize(levels, 8))
        for g in range(8):
            far = levels[np.abs(levels - a[p, g]) >= 10]
            a[p, g + 8] = far[np.random.randint(len(far))]
    return np.exp2(a.ravel()).repeat(32)


def f64(x):
    return np.asarray(x).astype(np.float64)


def striped(idx):
    return np.tile(idx.reshape(-1, 16).T, (8, 1)).astype(np.uint16)


def unstriped(offs):
    return offs[:16].T.reshape(-1).astype(np.int64)


E2M1 = np.array([0.0, 0.5, 1.0, 1.5, 2.0, 3.0, 4.0, 6.0, -0.0, -0.5, -1.0, -1.5, -2.0, -3.0, -4.0, -6.0])


def pack_weight(w, fmt):
    k, n = w.shape
    w = f64(np.asarray(w, np.float32).astype(ml_dtypes.bfloat16)).reshape(k // 32, 32, n)
    amax = np.abs(w).max(1)
    if fmt == "e4m3":
        byte = np.frexp(amax)[1] - 1 + 127 - 7
    else:
        mant, ex = np.frexp(amax / 6.0)
        byte = np.where(mant > 0.5, ex, ex - 1) + 127
    byte = np.clip(np.where(amax > 0, byte, 1), 1, 254)
    scaled = (w * np.exp2(127.0 - byte)[:, None, :]).reshape(k, n).astype(np.float32)
    by_word = np.ascontiguousarray(scaled.reshape(k // 512, 128, 4, n).transpose(0, 1, 3, 2))
    if fmt == "e4m3":
        words = by_word.astype(ml_dtypes.float8_e4m3fn).view(np.uint8)
    else:
        c = by_word.astype(ml_dtypes.float4_e2m1fn).view(np.uint8) & 0xF
        words = (c[..., 0::2] | (c[..., 1::2] << 4)).reshape(k // 512, 128, 2 * n)
    return np.ascontiguousarray(words), np.ascontiguousarray(byte.astype(np.uint8).reshape(k // 512, 16, n))


def unpack_weight(words, scales, fmt):
    g, _, n = scales.shape
    words = np.ascontiguousarray(words).reshape(g, 128, n, -1)
    if fmt == "e4m3":
        vals = words.view(ml_dtypes.float8_e4m3fn).astype(np.float64)
    else:
        nib = np.empty((g, 128, n, 4), np.uint8)
        nib[..., 0::2] = words & 0xF
        nib[..., 1::2] = words >> 4
        vals = E2M1[nib]
    vals = vals * np.repeat(np.exp2(scales.astype(np.float64) - 127.0), 8, axis=1)[..., None]
    return vals.transpose(0, 1, 3, 2).reshape(g * 512, n)


def pack_table4(v):
    words, scales = pack_weight(v, "e2m1")
    g, t = words.shape[0] // 2, v.shape[1]
    return np.ascontiguousarray(words.reshape(g, 2, 128, t, 2).transpose(0, 2, 3, 1, 4).reshape(g, 128, t, 4)), scales


def unpack_table4(words, scales):
    g, _, t, _ = words.shape
    return unpack_weight(words.reshape(g, 128, t, 2, 2).transpose(0, 3, 1, 2, 4).reshape(2 * g, 128, 2 * t), scales, "e2m1")


def sigm(f):
    return 1.0 / (1.0 + np.exp(-np.maximum(f, -700.0)))


K, N, T, J = 1024, 512, 2048, 1024


def setup_inputs():
    n = np.random.standard_normal
    s = mx_kscale(K)[:, None]
    p_tab = pack_table4(n((K, T)) * s)
    p_wa = pack_weight(n((K, N)) / np.sqrt(2 * K) / s, "e2m1")
    p_wc = pack_weight(n((K, N)) / np.sqrt(K) / s, "e4m3")
    return {
        "tab_words": p_tab[0],
        "tab_scales": p_tab[1],
        "wa_words": p_wa[0],
        "wa_scales": p_wa[1],
        "wb": (n((K, N)) / np.sqrt(2 * K) / s).astype(np.float32),
        "wc_words": p_wc[0],
        "wc_scales": p_wc[1],
        "wo": (n((K, N)) / np.sqrt(K) / s).astype(np.float32),
        "rT": (n((N, T))).astype(np.float32),
        "wgo": np.tile(np.random.uniform(0.5, 2.0, J), (128, 1)).astype(np.float32),
        "offs": striped(np.random.permutation(T)[:J]),
        "offs2": striped(np.random.permutation(T)[:J]),
    }


def reference(tab_words, tab_scales, wa_words, wa_scales, wb, wc_words, wc_scales, wo, rT, wgo, offs, offs2):
    idx = unstriped(offs)
    idx2 = unstriped(offs2)
    tab_ = unpack_table4(tab_words, tab_scales)[:, idx]
    tabb_ = unpack_table4(tab_words, tab_scales)[:, idx2]
    wa_ = unpack_weight(wa_words, wa_scales, "e2m1")
    wb_ = mxq(f64(wb), 0, "e4m3")
    za = wa_.T @ tabb_ + wb_.T @ tab_
    eta = sigm(za)
    wc_ = unpack_weight(wc_words, wc_scales, "e4m3")
    ms = wc_.T @ tab_
    wo_ = mxq(f64(wo), 0, "e4m3")
    ow = wo_.T @ tabb_
    out = np.zeros((N, T))
    out[:, idx2] = f64(wgo)[0] * (ow + eta * ms + f64(rT)[:, idx2])
    return out

@@ -1,0 +1,232 @@
+from contextlib import ExitStack
+
+import concourse.mybir as mybir
+from concourse.masks import make_identity
+
+K, N, T, J = 1024, 512, 2048, 1024
+FLOPS = 2 * 4 * K * N * J
+
+F32 = mybir.dt.float32
+BF16 = mybir.dt.bfloat16
+I32 = mybir.dt.int32
+U32 = mybir.dt.uint32
+U16 = mybir.dt.uint16
+U8 = mybir.dt.uint8
+FP8X4 = mybir.dt.float8_e4m3fn_x4
+FP4X4 = mybir.dt.float4_e2m1fn_x4
+MULT = mybir.AluOpType.mult
+ADD = mybir.AluOpType.add
+SIGMOID = mybir.ActivationFunctionType.Sigmoid
+
+P = 128
+PACK = 4
+PASSES = K // (P * PACK)
+QUADS = 4
+ROWS = 4
+HALF = 512
+HALVES = J // HALF
+TILES = HALF // P
+BLOCKS = N // P
+CHUNKS = ((0,), (1,), (2, 3))
+PAGES = 2
+SHIFTED = 112
+DST, SRC = 0, 1
+SIDES = (DST, SRC)
+
+
+def tile_list_rgg_ownL_kernel(
+    tc, tab_words, tab_scales, wa_words, wa_scales, wb, wc_words, wc_scales, wo, rT, wgo, offs, offs2, out
+):
+    nc = tc.nc
+    with ExitStack() as ctx:
+        keep = ctx.enter_context(tc.tile_pool(name="keep", bufs=1))
+        ring = ctx.enter_context(tc.tile_pool(name="ring", bufs=2))
+        psum = ctx.enter_context(tc.psum_pool(name="psum", bufs=2))
+
+        dst_list = keep.tile([P, J // 16], U16, name="dst_list")
+        src_list = keep.tile([P, J // 16], U16, name="src_list")
+        lists = (dst_list, src_list)
+
+        def offsets(side, h):
+            return lists[side][:, h * HALF // 16 : (h + 1) * HALF // 16]
+
+        table_scales = keep.tile([P, T], U8, name="table_scales", align_bytes=64)
+        nc.vector.memset(table_scales[:].bitcast(I32), 0)
+        planes = keep.tile([P, 2 * PASSES * N + len(SIDES) * J], U8, name="planes", align_bytes=64)
+        nc.vector.memset(planes[:].bitcast(I32), 0)
+        given_scales = planes[:, 0 : 2 * PASSES * N].rearrange("p (w a n) -> p w a n", w=2, a=PASSES)
+        moved = planes[:, 2 * PASSES * N :].rearrange("p (h c) -> p h c", h=HALVES)
+        pages = []
+
+        def clear_page(tag):
+            page = keep.tile([P, T], F32, name="page%d" % len(pages), tag=tag, align_bytes=64)
+            nc.vector.memset(page[:].bitcast(I32), 0)
+            pages.append(page)
+
+        clear_page("page0")
+        ident = keep.tile([P, P], F32, name="ident")
+        make_identity(nc, ident[:])
+
+        floats = (wb, wo)
+        raw = {}
+
+        def load_floats(blocks):
+            for w, source in enumerate(floats):
+                for a in range(PASSES):
+                    name = "raw%d%d%d" % (w, blocks[0], a)
+                    t = keep.tile([P, PACK, len(blocks) * P], F32, name=name, tag=name)
+                    rows = source[a * P * PACK : (a + 1) * P * PACK, blocks[0] * P : (blocks[-1] + 1) * P]
+                    nc.sync.dma_start(t[:], rows.rearrange("(p i) n -> p i n", i=PACK))
+                    for b in blocks:
+                        raw[w, b, a] = t[:, :, (b - blocks[0]) * P : (b - blocks[0] + 1) * P]
+
+        def load_scales(w, scales):
+            for q in range(QUADS):
+                nc.sync.dma_start(
+                    given_scales[32 * q : 32 * q + ROWS, w, :, :].bitcast(I32),
+                    scales[:, ROWS * q : ROWS * (q + 1), :].rearrange("a r n -> r a n").bitcast(I32),
+                )
+
+        picked = {}
+
+        def pick_scales(h, tag):
+            g = keep.tile([P, len(SIDES) * HALF], U8, name="picked%d" % h, tag=tag, align_bytes=64)
+            for side in SIDES:
+                nc.vector.tensor_copy(g[:, side * HALF : (side + 1) * HALF], table_scales[:].indirect(offsets(side, h)))
+            nc.sync.dma_start(moved[0:SHIFTED, h, :].bitcast(I32), g[ROWS : ROWS + SHIFTED, :].bitcast(I32))
+            picked[h] = (g[:], moved[:, h, :])
+
+        parted = {}
+
+        def pick_words(h, tag):
+            both = keep.tile([P, len(SIDES), HALF], I32, name="both%d" % h, tag=tag, align_bytes=64)
+            for side in SIDES:
+                nc.vector.tensor_copy(both[:, side, :].bitcast(U32), table_words[:].bitcast(U32).indirect(offsets(side, h)))
+            for side in SIDES:
+                t = keep.tile([P, PASSES, 2 * HALF], U8, name="parted%d%d" % (side, h), align_bytes=64)
+                nc.vector.tensor_copy(
+                    t[:].bitcast(U16), both[:, side, :].bitcast(U16).rearrange("p (j a) -> p a j", a=PASSES)
+                )
+                parted[side, h] = t
+
+        made = {}
+
+        def quantize(b):
+            grouped = keep.tile([P, len(floats), PASSES, P * PACK], BF16, name="grouped%d" % b, tag="stage%d" % b, align_bytes=64)
+            for w in range(len(floats)):
+                for a in range(PASSES):
+                    nc.scalar.copy(
+                        grouped[:, w, a, :].rearrange("p (c m i) -> p c i m", m=4, i=PACK),
+                        raw[w, b, a].rearrange("p i (c m) -> p c i m", m=4),
+                    )
+            codes = keep.tile([P, len(floats), PASSES, P], U32, name="codes%d" % b, align_bytes=64)
+            scales = keep.tile([P, len(floats), PASSES, P], U8, name="scales%d" % b, align_bytes=64)
+            nc.vector.quantize_mx(
+                out=codes[:].rearrange("p w a n -> p (w a n)").bitcast(FP8X4),
+                scales=scales[:].rearrange("p w a n -> p (w a n)"),
+                in_=grouped[:].rearrange("p w a n -> p (w a n)"),
+            )
+            made[b] = (codes, scales)
+
+        nc.sync.dma_start(dst_list[:], offs2)
+        nc.sync.dma_start(src_list[:], offs)
+        for q in range(QUADS):
+            nc.sync.dma_start(
+                table_scales[32 * q : 32 * q + PASSES * ROWS, :].bitcast(I32),
+                tab_scales[:, ROWS * q : ROWS * (q + 1), :].bitcast(I32),
+            )
+        table_words = keep.tile([P, T], I32, name="table_words", align_bytes=64)
+        nc.sync.dma_start(table_words[:], tab_words[0].rearrange("p t b -> p (t b)").bitcast(I32))
+        load_floats(CHUNKS[0])
+        wa_codes = keep.tile([P, PASSES, 2 * N], U8, name="wa_codes", align_bytes=64)
+        nc.sync.dma_start(wa_codes[:].bitcast(I32), wa_words.rearrange("a p c -> p a c").bitcast(I32))
+        load_scales(0, wa_scales)
+        pick_scales(0, "picked0")
+        wc_codes = keep.tile([P, PASSES, N], I32, name="wc_codes", align_bytes=64)
+        nc.sync.dma_start(wc_codes[:], wc_words.rearrange("a p n i -> p a (n i)").bitcast(I32))
+        load_floats(CHUNKS[1])
+        load_scales(1, wc_scales)
+        pick_words(0, "both0")
+        quantize(0)
+        pick_scales(1, "stage0")
+        quantize(1)
+        pick_words(1, "stage1")
+        clear_page("stage1")
+
+        states = [keep.tile([P, T], F32, name="state%d" % b) for b in range(BLOCKS)]
+        nc.sync.dma_start(states[0][:], rT[0:P, :])
+        edge_weight = keep.tile([P, J], F32, name="edge_weight")
+        nc.sync.dma_start(edge_weight[:], wgo)
+        nc.sync.dma_start(states[1][:], rT[P : 2 * P, :])
+        load_floats(CHUNKS[2])
+        for b in range(2, BLOCKS):
+            nc.sync.dma_start(states[b][:], rT[b * P : (b + 1) * P, :])
+
+        def weight(w, a, b):
+            cols = slice(b * P, (b + 1) * P)
+            if w == "wa":
+                return wa_codes[:, a, 2 * b * P : 2 * (b + 1) * P].bitcast(FP4X4), given_scales[:, 0, a, cols]
+            if w == "wc":
+                return wc_codes[:, a, cols].bitcast(FP8X4), given_scales[:, 1, a, cols]
+            codes, scales = made[b]
+            f = ("wb", "wo").index(w)
+            return codes[:, f, a, :].bitcast(FP8X4), scales[:, f, a, :]
+
+        def product(name, terms, b, h):
+            bank = psum.tile([P, TILES, P], F32, name=name)
+            steps = [(w, side, a) for w, side in terms for a in range(PASSES)]
+            for e in range(TILES):
+                for s, (w, side, a) in enumerate(steps):
+                    codes, scales = weight(w, a, b)
+                    first = side * HALF + e * P
+                    nc.tensor.matmul_mx(
+                        out=bank[:, e, :],
+                        lhsT=parted[side, h][:, a, 2 * e * P : 2 * (e + 1) * P].bitcast(FP4X4),
+                        lhsT_scale=picked[h][a][:, first : first + P],
+                        rhs=codes,
+                        rhs_scale=scales,
+                        start=(s == 0),
+                        stop=(s == len(steps) - 1),
+                    )
+            return bank
+
+        def multiply(b, h):
+            if (b, h) == (0, 0):
+                drawn = keep.tile([P, 2, TILES, P], F32, name="first_drawn", tag="raw111")
+            else:
+                drawn = ring.tile([P, 2, TILES, P], F32, name="drawn")
+            gate, own = drawn[:, 0], drawn[:, 1]
+            gate_sum = product("gate_sum", (("wb", SRC), ("wa", DST)), b, h)
+            nc.scalar.activation(gate, gate_sum[:], SIGMOID)
+            own_sum = product("own_sum", (("wo", DST),), b, h)
+            nc.scalar.copy(own, own_sum[:])
+            message = product("message", (("wc", SRC),), b, h)
+            gated = ring.tile([P, TILES, P], F32, name="gated")
+            nc.vector.tensor_tensor(gated[:], message[:], gate, MULT)
+            return gated, own
+
+        def place(b, h, gated, own):
+            turned = psum.tile([P, TILES, P], F32, name="turned")
+            for e in range(TILES):
+                nc.tensor.matmul(turned[:, e, :], lhsT=own[:, e, :], rhs=ident[:], is_transpose=True, start=True, stop=False)
+                nc.tensor.matmul(turned[:, e, :], lhsT=gated[:, e, :], rhs=ident[:], is_transpose=True, start=False, stop=True)
+            update = ring.tile([P, HALF], F32, name="update")
+            nc.scalar.copy(update[:], turned[:].rearrange("p e j -> p (e j)"))
+            total = ring.tile([P, HALF], F32, name="total")
+            nc.vector.tensor_tensor(total[:], states[b][:].indirect(offsets(DST, h)), update[:], ADD)
+            page = pages[b % PAGES]
+            nc.vector.tensor_tensor(
+                page[:].indirect(offsets(DST, h)), total[:], edge_weight[:, h * HALF : (h + 1) * HALF], MULT
+            )
+            if h == HALVES - 1:
+                nc.sync.dma_start(out[b * P : (b + 1) * P, :], page[:])
+
+        units = [(pair + b, h) for pair in range(0, BLOCKS, PAGES) for h in range(HALVES) for b in range(PAGES)]
+        ahead = multiply(*units[0])
+        for u, unit in enumerate(units):
+            ready = ahead
+            if u + 1 < len(units):
+                if units[u + 1][0] not in made:
+                    quantize(units[u + 1][0])
+                ahead = multiply(*units[u + 1])
+            place(*unit, *ready)

@@ -25,9 +25,7 @@ QUADS = 4
 ROWS = 4
 HALF = 512
 HALVES = J // HALF
-TILES = HALF // P
 BLOCKS = N // P
-CHUNKS = ((0,), (1,), (2, 3))
 PAGES = 2
 SHIFTED = 112
 DST, SRC = 0, 1
@@ -47,23 +45,24 @@ def tile_list_rgg_ownL_kernel(
         src_list = keep.tile([P, J // 16], U16, name="src_list")
         lists = (dst_list, src_list)
 
-        def offsets(side, h):
-            return lists[side][:, h * HALF // 16 : (h + 1) * HALF // 16]
+        def offsets(side, first, count):
+            return lists[side][:, first // 16 : (first + count) // 16]
 
         table_scales = keep.tile([P, T], U8, name="table_scales", align_bytes=64)
-        nc.vector.memset(table_scales[:].bitcast(I32), 0)
+        nc.gpsimd.memset(table_scales[:].bitcast(I32), 0)
         planes = keep.tile([P, 2 * PASSES * N + len(SIDES) * J], U8, name="planes", align_bytes=64)
         nc.vector.memset(planes[:].bitcast(I32), 0)
         given_scales = planes[:, 0 : 2 * PASSES * N].rearrange("p (w a n) -> p w a n", w=2, a=PASSES)
-        moved = planes[:, 2 * PASSES * N :].rearrange("p (h c) -> p h c", h=HALVES)
+        moved = planes[:, 2 * PASSES * N :]
         pages = []
 
-        def clear_page(tag):
-            page = keep.tile([P, T], F32, name="page%d" % len(pages), tag=tag, align_bytes=64)
+        def clear_page():
+            name = "page%d" % len(pages)
+            page = keep.tile([P, T], F32, name=name, tag=name)
             nc.vector.memset(page[:].bitcast(I32), 0)
             pages.append(page)
 
-        clear_page("page0")
+        clear_page()
         ident = keep.tile([P, P], F32, name="ident")
         make_identity(nc, ident[:])
 
@@ -73,8 +72,7 @@ def tile_list_rgg_ownL_kernel(
         def load_floats(blocks):
             for w, source in enumerate(floats):
                 for a in range(PASSES):
-                    name = "raw%d%d%d" % (w, blocks[0], a)
-                    t = keep.tile([P, PACK, len(blocks) * P], F32, name=name, tag=name)
+                    t = keep.tile([P, PACK, len(blocks) * P], F32, name="raw%d%d%d" % (w, blocks[0], a))
                     rows = source[a * P * PACK : (a + 1) * P * PACK, blocks[0] * P : (blocks[-1] + 1) * P]
                     nc.sync.dma_start(t[:], rows.rearrange("(p i) n -> p i n", i=PACK))
                     for b in blocks:
@@ -87,25 +85,17 @@ def tile_list_rgg_ownL_kernel(
                     scales[:, ROWS * q : ROWS * (q + 1), :].rearrange("a r n -> r a n").bitcast(I32),
                 )
 
-        picked = {}
-
-        def pick_scales(h, tag):
-            g = keep.tile([P, len(SIDES) * HALF], U8, name="picked%d" % h, tag=tag, align_bytes=64)
-            for side in SIDES:
-                nc.vector.tensor_copy(g[:, side * HALF : (side + 1) * HALF], table_scales[:].indirect(offsets(side, h)))
-            nc.sync.dma_start(moved[0:SHIFTED, h, :].bitcast(I32), g[ROWS : ROWS + SHIFTED, :].bitcast(I32))
-            picked[h] = (g[:], moved[:, h, :])
-
         parted = {}
 
         def pick_words(h, tag):
-            both = keep.tile([P, len(SIDES), HALF], I32, name="both%d" % h, tag=tag, align_bytes=64)
+            both = keep.tile([P, len(SIDES) * HALF], I32, name="both%d" % h, tag=tag, align_bytes=64)
             for side in SIDES:
-                nc.vector.tensor_copy(both[:, side, :].bitcast(U32), table_words[:].bitcast(U32).indirect(offsets(side, h)))
+                window = table_words[:].bitcast(U32)
+                nc.vector.tensor_copy(both[:, side * HALF : (side + 1) * HALF].bitcast(U32), window.indirect(offsets(side, h * HALF, HALF)))
             for side in SIDES:
                 t = keep.tile([P, PASSES, 2 * HALF], U8, name="parted%d%d" % (side, h), align_bytes=64)
                 nc.vector.tensor_copy(
-                    t[:].bitcast(U16), both[:, side, :].bitcast(U16).rearrange("p (j a) -> p a j", a=PASSES)
+                    t[:].bitcast(U16), both[:, side * HALF : (side + 1) * HALF].bitcast(U16).rearrange("p (j a) -> p a j", a=PASSES)
                 )
                 parted[side, h] = t
 
@@ -137,30 +127,30 @@ def tile_list_rgg_ownL_kernel(
             )
         table_words = keep.tile([P, T], I32, name="table_words", align_bytes=64)
         nc.sync.dma_start(table_words[:], tab_words[0].rearrange("p t b -> p (t b)").bitcast(I32))
-        load_floats(CHUNKS[0])
+        load_floats((0,))
         wa_codes = keep.tile([P, PASSES, 2 * N], U8, name="wa_codes", align_bytes=64)
         nc.sync.dma_start(wa_codes[:].bitcast(I32), wa_words.rearrange("a p c -> p a c").bitcast(I32))
         load_scales(0, wa_scales)
-        pick_scales(0, "picked0")
         wc_codes = keep.tile([P, PASSES, N], I32, name="wc_codes", align_bytes=64)
         nc.sync.dma_start(wc_codes[:], wc_words.rearrange("a p n i -> p a (n i)").bitcast(I32))
-        load_floats(CHUNKS[1])
         load_scales(1, wc_scales)
-        pick_words(0, "both0")
-        quantize(0)
-        pick_scales(1, "stage0")
-        quantize(1)
-        pick_words(1, "stage1")
-        clear_page("stage1")
-
+        picked = keep.tile([P, len(SIDES) * J], U8, name="picked", align_bytes=64)
+        for side in SIDES:
+            nc.vector.tensor_copy(picked[:, side * J : (side + 1) * J], table_scales[:].indirect(lists[side][:]))
+        nc.sync.dma_start(moved[0:SHIFTED, :].bitcast(I32), picked[ROWS : ROWS + SHIFTED, :].bitcast(I32))
+        edge_scales = (picked[:], moved)
+        load_floats((1,))
         states = [keep.tile([P, T], F32, name="state%d" % b) for b in range(BLOCKS)]
         nc.sync.dma_start(states[0][:], rT[0:P, :])
         edge_weight = keep.tile([P, J], F32, name="edge_weight")
         nc.sync.dma_start(edge_weight[:], wgo)
-        nc.sync.dma_start(states[1][:], rT[P : 2 * P, :])
-        load_floats(CHUNKS[2])
-        for b in range(2, BLOCKS):
+        load_floats((2, 3))
+        for b in range(1, BLOCKS):
             nc.sync.dma_start(states[b][:], rT[b * P : (b + 1) * P, :])
+
+        pick_words(0, "both0")
+        quantize(0)
+        pick_words(1, "stage0")
 
         def weight(w, a, b):
             cols = slice(b * P, (b + 1) * P)
@@ -172,61 +162,74 @@ def tile_list_rgg_ownL_kernel(
             f = ("wb", "wo").index(w)
             return codes[:, f, a, :].bitcast(FP8X4), scales[:, f, a, :]
 
-        def product(name, terms, b, h):
-            bank = psum.tile([P, TILES, P], F32, name=name)
+        def product(name, terms, unit):
+            b, first, count = unit
+            bank = psum.tile([P, HALF], F32, name=name)
             steps = [(w, side, a) for w, side in terms for a in range(PASSES)]
-            for e in range(TILES):
+            for e in range(0, count, P):
+                h, j = divmod(first + e, HALF)
                 for s, (w, side, a) in enumerate(steps):
                     codes, scales = weight(w, a, b)
-                    first = side * HALF + e * P
+                    column = side * J + first + e
                     nc.tensor.matmul_mx(
-                        out=bank[:, e, :],
-                        lhsT=parted[side, h][:, a, 2 * e * P : 2 * (e + 1) * P].bitcast(FP4X4),
-                        lhsT_scale=picked[h][a][:, first : first + P],
+                        out=bank[:, e : e + P],
+                        lhsT=parted[side, h][:, a, 2 * j : 2 * (j + P)].bitcast(FP4X4),
+                        lhsT_scale=edge_scales[a][:, column : column + P],
                         rhs=codes,
                         rhs_scale=scales,
                         start=(s == 0),
                         stop=(s == len(steps) - 1),
                     )
-            return bank
+            return bank[:, 0:count]
 
-        def multiply(b, h):
-            if (b, h) == (0, 0):
-                drawn = keep.tile([P, 2, TILES, P], F32, name="first_drawn", tag="raw111")
-            else:
-                drawn = ring.tile([P, 2, TILES, P], F32, name="drawn")
-            gate, own = drawn[:, 0], drawn[:, 1]
-            gate_sum = product("gate_sum", (("wb", SRC), ("wa", DST)), b, h)
-            nc.scalar.activation(gate, gate_sum[:], SIGMOID)
-            own_sum = product("own_sum", (("wo", DST),), b, h)
-            nc.scalar.copy(own, own_sum[:])
-            message = product("message", (("wc", SRC),), b, h)
-            gated = ring.tile([P, TILES, P], F32, name="gated")
-            nc.vector.tensor_tensor(gated[:], message[:], gate, MULT)
+        def multiply(unit, gate):
+            count = unit[2]
+            if unit[0] not in made:
+                quantize(unit[0])
+            gate_sum = product("gate_sum", (("wb", SRC), ("wa", DST)), unit)
+            nc.scalar.activation(gate[:, 0:count], gate_sum, SIGMOID)
+            own_sum = product("own_sum", (("wo", DST),), unit)
+            own = ring.tile([P, HALF], F32, name="own")
+            nc.scalar.copy(own[:, 0:count], own_sum)
+            return product("message", (("wc", SRC),), unit), gate[:, 0:count], own
+
+        def let_through(gated, sums):
+            message, gate, own = sums
+            nc.vector.tensor_tensor(gated[:, 0 : gate.shape[1]], message, gate, MULT)
             return gated, own
 
-        def place(b, h, gated, own):
-            turned = psum.tile([P, TILES, P], F32, name="turned")
-            for e in range(TILES):
-                nc.tensor.matmul(turned[:, e, :], lhsT=own[:, e, :], rhs=ident[:], is_transpose=True, start=True, stop=False)
-                nc.tensor.matmul(turned[:, e, :], lhsT=gated[:, e, :], rhs=ident[:], is_transpose=True, start=False, stop=True)
+        def turn(unit, gated, own):
+            count = unit[2]
+            turned = psum.tile([P, HALF], F32, name="turned")
+            for e in range(0, count, P):
+                cols = slice(e, e + P)
+                nc.tensor.matmul(turned[:, cols], lhsT=own[:, cols], rhs=ident[:], is_transpose=True, start=True, stop=False)
+                nc.tensor.matmul(turned[:, cols], lhsT=gated[:, cols], rhs=ident[:], is_transpose=True, start=False, stop=True)
             update = ring.tile([P, HALF], F32, name="update")
-            nc.scalar.copy(update[:], turned[:].rearrange("p e j -> p (e j)"))
-            total = ring.tile([P, HALF], F32, name="total")
-            nc.vector.tensor_tensor(total[:], states[b][:].indirect(offsets(DST, h)), update[:], ADD)
-            page = pages[b % PAGES]
-            nc.vector.tensor_tensor(
-                page[:].indirect(offsets(DST, h)), total[:], edge_weight[:, h * HALF : (h + 1) * HALF], MULT
-            )
-            if h == HALVES - 1:
-                nc.sync.dma_start(out[b * P : (b + 1) * P, :], page[:])
+            nc.scalar.copy(update[:, 0:count], turned[:, 0:count])
+            return update
 
-        units = [(pair + b, h) for pair in range(0, BLOCKS, PAGES) for h in range(HALVES) for b in range(PAGES)]
-        ahead = multiply(*units[0])
+        def fresh_gate():
+            return ring.tile([P, HALF], F32, name="gate")
+
+        units = [(b, first, HALF) for b in range(BLOCKS) for first in range(0, J, HALF)]
+        units[0:1] = [(0, first, HALF // 2) for first in range(0, HALF, HALF // 2)]
+
+        sums = multiply(units[0], keep.tile([P, HALF], F32, name="first_gate", tag="page1"))
+        terms = let_through(keep.tile([P, HALF], F32, name="first_gated"), sums)
+        clear_page()
+        sums = multiply(units[1], fresh_gate())
         for u, unit in enumerate(units):
-            ready = ahead
+            b, first, count = unit
+            update = turn(unit, *terms)
+            total = ring.tile([P, HALF], F32, name="total")
+            listed = offsets(DST, first, count)
+            nc.vector.tensor_tensor(total[:, 0:count], states[b][:].indirect(listed), update[:, 0:count], ADD)
             if u + 1 < len(units):
-                if units[u + 1][0] not in made:
-                    quantize(units[u + 1][0])
-                ahead = multiply(*units[u + 1])
-            place(*unit, *ready)
+                terms = let_through(update, sums)
+            page = pages[b % PAGES]
+            nc.vector.tensor_tensor(page[:].indirect(listed), total[:, 0:count], edge_weight[:, first : first + count], MULT)
+            if first + count == J:
+                nc.sync.dma_start(out[b * P : (b + 1) * P, :], page[:])
+            if u + 2 < len(units):
+                sums = multiply(units[u + 2], fresh_gate())

@@ -85,6 +85,17 @@ def tile_list_rgg_ownL_kernel(
                     scales[:, ROWS * q : ROWS * (q + 1), :].rearrange("a r n -> r a n").bitcast(I32),
                 )
 
+        given_codes = {}
+
+        def load_codes(blocks):
+            sources = (("wa", wa_words.rearrange("a p c -> p a c"), 2), ("wc", wc_words.rearrange("a p n i -> p a (n i)"), 4))
+            for w, words, size in sources:
+                width = size * P
+                t = keep.tile([P, PASSES, len(blocks) * width], U8, name="%s_codes%d" % (w, blocks[0]), align_bytes=64)
+                nc.sync.dma_start(t[:].bitcast(I32), words[:, :, blocks[0] * width : (blocks[-1] + 1) * width].bitcast(I32))
+                for b in blocks:
+                    given_codes[w, b] = t[:, :, (b - blocks[0]) * width : (b - blocks[0] + 1) * width]
+
         parted = {}
 
         def pick_words(h, tag):
@@ -127,13 +138,10 @@ def tile_list_rgg_ownL_kernel(
             )
         table_words = keep.tile([P, T], I32, name="table_words", align_bytes=64)
         nc.sync.dma_start(table_words[:], tab_words[0].rearrange("p t b -> p (t b)").bitcast(I32))
-        load_floats((0,))
-        wa_codes = keep.tile([P, PASSES, 2 * N], U8, name="wa_codes", align_bytes=64)
-        nc.sync.dma_start(wa_codes[:].bitcast(I32), wa_words.rearrange("a p c -> p a c").bitcast(I32))
         load_scales(0, wa_scales)
-        wc_codes = keep.tile([P, PASSES, N], I32, name="wc_codes", align_bytes=64)
-        nc.sync.dma_start(wc_codes[:], wc_words.rearrange("a p n i -> p a (n i)").bitcast(I32))
+        load_floats((0,))
         load_scales(1, wc_scales)
+        load_codes(range(0, 1))
         picked = keep.tile([P, len(SIDES) * J], U8, name="picked", align_bytes=64)
         for side in SIDES:
             nc.vector.tensor_copy(picked[:, side * J : (side + 1) * J], table_scales[:].indirect(lists[side][:]))
@@ -142,10 +150,13 @@ def tile_list_rgg_ownL_kernel(
         load_floats((1,))
         states = [keep.tile([P, T], F32, name="state%d" % b) for b in range(BLOCKS)]
         nc.sync.dma_start(states[0][:], rT[0:P, :])
-        edge_weight = keep.tile([P, J], F32, name="edge_weight")
-        nc.sync.dma_start(edge_weight[:], wgo)
+        edge_weight = [keep.tile([P, HALF], F32, name="edge_weight%d" % h) for h in range(HALVES)]
+        nc.sync.dma_start(edge_weight[0][:], wgo[:, 0:HALF])
+        load_codes(range(1, BLOCKS))
+        nc.sync.dma_start(edge_weight[1][:], wgo[:, HALF:J])
+        nc.sync.dma_start(states[1][:], rT[P : 2 * P, :])
         load_floats((2, 3))
-        for b in range(1, BLOCKS):
+        for b in range(2, BLOCKS):
             nc.sync.dma_start(states[b][:], rT[b * P : (b + 1) * P, :])
 
         pick_words(0, "both0")
@@ -155,9 +166,9 @@ def tile_list_rgg_ownL_kernel(
         def weight(w, a, b):
             cols = slice(b * P, (b + 1) * P)
             if w == "wa":
-                return wa_codes[:, a, 2 * b * P : 2 * (b + 1) * P].bitcast(FP4X4), given_scales[:, 0, a, cols]
+                return given_codes[w, b][:, a, :].bitcast(FP4X4), given_scales[:, 0, a, cols]
             if w == "wc":
-                return wc_codes[:, a, cols].bitcast(FP8X4), given_scales[:, 1, a, cols]
+                return given_codes[w, b][:, a, :].bitcast(FP8X4), given_scales[:, 1, a, cols]
             codes, scales = made[b]
             f = ("wb", "wo").index(w)
             return codes[:, f, a, :].bitcast(FP8X4), scales[:, f, a, :]
@@ -165,7 +176,7 @@ def tile_list_rgg_ownL_kernel(
         def product(name, terms, unit):
             b, first, count = unit
             bank = psum.tile([P, HALF], F32, name=name)
-            steps = [(w, side, a) for w, side in terms for a in range(PASSES)]
+            steps = [(w, side, a) for w, side in terms for a in reversed(range(PASSES))]
             for e in range(0, count, P):
                 h, j = divmod(first + e, HALF)
                 for s, (w, side, a) in enumerate(steps):
@@ -203,8 +214,8 @@ def tile_list_rgg_ownL_kernel(
             turned = psum.tile([P, HALF], F32, name="turned")
             for e in range(0, count, P):
                 cols = slice(e, e + P)
-                nc.tensor.matmul(turned[:, cols], lhsT=own[:, cols], rhs=ident[:], is_transpose=True, start=True, stop=False)
-                nc.tensor.matmul(turned[:, cols], lhsT=gated[:, cols], rhs=ident[:], is_transpose=True, start=False, stop=True)
+                nc.tensor.matmul(turned[:, cols], lhsT=gated[:, cols], rhs=ident[:], is_transpose=True, start=True, stop=False)
+                nc.tensor.matmul(turned[:, cols], lhsT=own[:, cols], rhs=ident[:], is_transpose=True, start=False, stop=True)
             update = ring.tile([P, HALF], F32, name="update")
             nc.scalar.copy(update[:, 0:count], turned[:, 0:count])
             return update
@@ -228,7 +239,8 @@ def tile_list_rgg_ownL_kernel(
             if u + 1 < len(units):
                 terms = let_through(update, sums)
             page = pages[b % PAGES]
-            nc.vector.tensor_tensor(page[:].indirect(listed), total[:, 0:count], edge_weight[:, first : first + count], MULT)
+            h, j = divmod(first, HALF)
+            nc.vector.tensor_tensor(page[:].indirect(listed), total[:, 0:count], edge_weight[h][:, j : j + count], MULT)
             if first + count == J:
                 nc.sync.dma_start(out[b * P : (b + 1) * P, :], page[:])
             if u + 2 < len(units):

@@ -22,12 +22,15 @@ P = 128
 PACK = 4
 PASSES = K // (P * PACK)
 QUADS = 4
+QUAD = P // QUADS
 ROWS = 4
+STRIPE = 16
+LINE = 4
 HALF = 512
 HALVES = J // HALF
 BLOCKS = N // P
 PAGES = 2
-SHIFTED = 112
+MOVED_ROWS = 112
 DST, SRC = 0, 1
 SIDES = (DST, SRC)
 
@@ -41,19 +44,20 @@ def tile_list_rgg_ownL_kernel(
         ring = ctx.enter_context(tc.tile_pool(name="ring", bufs=2))
         psum = ctx.enter_context(tc.psum_pool(name="psum", bufs=2))
 
-        dst_list = keep.tile([P, J // 16], U16, name="dst_list")
-        src_list = keep.tile([P, J // 16], U16, name="src_list")
+        dst_list = keep.tile([P, J // STRIPE], U16, name="dst_list")
+        src_list = keep.tile([P, J // STRIPE], U16, name="src_list")
         lists = (dst_list, src_list)
 
         def offsets(side, first, count):
-            return lists[side][:, first // 16 : (first + count) // 16]
+            return lists[side][:, first // STRIPE : (first + count) // STRIPE]
 
         table_scales = keep.tile([P, T], U8, name="table_scales", align_bytes=64)
         nc.gpsimd.memset(table_scales[:].bitcast(I32), 0)
         planes = keep.tile([P, 2 * PASSES * N + len(SIDES) * J], U8, name="planes", align_bytes=64)
         nc.vector.memset(planes[:].bitcast(I32), 0)
         given_scales = planes[:, 0 : 2 * PASSES * N].rearrange("p (w a n) -> p w a n", w=2, a=PASSES)
-        moved = planes[:, 2 * PASSES * N :]
+        moved_scales = planes[:, 2 * PASSES * N :]
+
         pages = []
 
         def clear_page():
@@ -66,29 +70,31 @@ def tile_list_rgg_ownL_kernel(
         ident = keep.tile([P, P], F32, name="ident")
         make_identity(nc, ident[:])
 
-        floats = (wb, wo)
+        float_weights = (wb, wo)
         raw = {}
 
-        def load_floats(blocks):
-            for w, source in enumerate(floats):
+        def load_floats(b):
+            for w, source in enumerate(float_weights):
                 for a in range(PASSES):
-                    t = keep.tile([P, PACK, len(blocks) * P], F32, name="raw%d%d%d" % (w, blocks[0], a))
-                    rows = source[a * P * PACK : (a + 1) * P * PACK, blocks[0] * P : (blocks[-1] + 1) * P]
+                    t = keep.tile([P, PACK, P], F32, name="raw%d%d%d" % (w, b, a))
+                    rows = source[a * P * PACK : (a + 1) * P * PACK, b * P : (b + 1) * P]
                     nc.sync.dma_start(t[:], rows.rearrange("(p i) n -> p i n", i=PACK))
-                    for b in blocks:
-                        raw[w, b, a] = t[:, :, (b - blocks[0]) * P : (b - blocks[0] + 1) * P]
+                    raw[w, b, a] = t
 
         def load_scales(w, scales):
             for q in range(QUADS):
                 nc.sync.dma_start(
-                    given_scales[32 * q : 32 * q + ROWS, w, :, :].bitcast(I32),
+                    given_scales[QUAD * q : QUAD * q + ROWS, w, :, :].bitcast(I32),
                     scales[:, ROWS * q : ROWS * (q + 1), :].rearrange("a r n -> r a n").bitcast(I32),
                 )
 
         given_codes = {}
 
         def load_codes(blocks):
-            sources = (("wa", wa_words.rearrange("a p c -> p a c"), 2), ("wc", wc_words.rearrange("a p n i -> p a (n i)"), 4))
+            sources = (
+                ("wa", wa_words.rearrange("a p c -> p a c"), 2),
+                ("wc", wc_words.rearrange("a p n i -> p a (n i)"), 4),
+            )
             for w, words, size in sources:
                 width = size * P
                 t = keep.tile([P, PASSES, len(blocks) * width], U8, name="%s_codes%d" % (w, blocks[0]), align_bytes=64)
@@ -102,30 +108,32 @@ def tile_list_rgg_ownL_kernel(
             both = keep.tile([P, len(SIDES) * HALF], I32, name="both%d" % h, tag=tag, align_bytes=64)
             for side in SIDES:
                 window = table_words[:].bitcast(U32)
-                nc.vector.tensor_copy(both[:, side * HALF : (side + 1) * HALF].bitcast(U32), window.indirect(offsets(side, h * HALF, HALF)))
+                nc.vector.tensor_copy(
+                    both[:, side * HALF : (side + 1) * HALF].bitcast(U32), window.indirect(offsets(side, h * HALF, HALF))
+                )
             for side in SIDES:
                 t = keep.tile([P, PASSES, 2 * HALF], U8, name="parted%d%d" % (side, h), align_bytes=64)
-                nc.vector.tensor_copy(
-                    t[:].bitcast(U16), both[:, side * HALF : (side + 1) * HALF].bitcast(U16).rearrange("p (j a) -> p a j", a=PASSES)
-                )
+                pairs = both[:, side * HALF : (side + 1) * HALF].bitcast(U16)
+                nc.vector.tensor_copy(t[:].bitcast(U16), pairs.rearrange("p (j a) -> p a j", a=PASSES))
                 parted[side, h] = t
 
         made = {}
 
         def quantize(b):
-            grouped = keep.tile([P, len(floats), PASSES, P * PACK], BF16, name="grouped%d" % b, tag="stage%d" % b, align_bytes=64)
-            for w in range(len(floats)):
+            shape = [P, len(float_weights), PASSES, P]
+            grouped = keep.tile(shape + [PACK], BF16, name="grouped%d" % b, tag="stage%d" % b, align_bytes=64)
+            for w in range(len(float_weights)):
                 for a in range(PASSES):
                     nc.scalar.copy(
-                        grouped[:, w, a, :].rearrange("p (c m i) -> p c i m", m=4, i=PACK),
-                        raw[w, b, a].rearrange("p i (c m) -> p c i m", m=4),
+                        grouped[:, w, a].rearrange("p (c m) i -> p c i m", m=LINE),
+                        raw[w, b, a][:].rearrange("p i (c m) -> p c i m", m=LINE),
                     )
-            codes = keep.tile([P, len(floats), PASSES, P], U32, name="codes%d" % b, align_bytes=64)
-            scales = keep.tile([P, len(floats), PASSES, P], U8, name="scales%d" % b, align_bytes=64)
+            codes = keep.tile(shape, U32, name="codes%d" % b, align_bytes=64)
+            scales = keep.tile(shape, U8, name="scales%d" % b, align_bytes=64)
             nc.vector.quantize_mx(
                 out=codes[:].rearrange("p w a n -> p (w a n)").bitcast(FP8X4),
                 scales=scales[:].rearrange("p w a n -> p (w a n)"),
-                in_=grouped[:].rearrange("p w a n -> p (w a n)"),
+                in_=grouped[:].rearrange("p w a n i -> p (w a n i)"),
             )
             made[b] = (codes, scales)
 
@@ -133,31 +141,40 @@ def tile_list_rgg_ownL_kernel(
         nc.sync.dma_start(src_list[:], offs)
         for q in range(QUADS):
             nc.sync.dma_start(
-                table_scales[32 * q : 32 * q + PASSES * ROWS, :].bitcast(I32),
+                table_scales[QUAD * q : QUAD * q + PASSES * ROWS, :].bitcast(I32),
                 tab_scales[:, ROWS * q : ROWS * (q + 1), :].bitcast(I32),
             )
         table_words = keep.tile([P, T], I32, name="table_words", align_bytes=64)
         nc.sync.dma_start(table_words[:], tab_words[0].rearrange("p t b -> p (t b)").bitcast(I32))
         load_scales(0, wa_scales)
-        load_floats((0,))
+        load_floats(0)
         load_scales(1, wc_scales)
         load_codes(range(0, 1))
-        picked = keep.tile([P, len(SIDES) * J], U8, name="picked", align_bytes=64)
+
+        picked_scales = keep.tile([P, len(SIDES) * J], U8, name="picked_scales", align_bytes=64)
         for side in SIDES:
-            nc.vector.tensor_copy(picked[:, side * J : (side + 1) * J], table_scales[:].indirect(lists[side][:]))
-        nc.sync.dma_start(moved[0:SHIFTED, :].bitcast(I32), picked[ROWS : ROWS + SHIFTED, :].bitcast(I32))
-        edge_scales = (picked[:], moved)
-        load_floats((1,))
+            nc.vector.tensor_copy(picked_scales[:, side * J : (side + 1) * J], table_scales[:].indirect(lists[side][:]))
+        nc.sync.dma_start(
+            moved_scales[0:MOVED_ROWS, :].bitcast(I32), picked_scales[ROWS : ROWS + MOVED_ROWS, :].bitcast(I32)
+        )
+        edge_scales = (picked_scales[:], moved_scales)
+
         states = [keep.tile([P, T], F32, name="state%d" % b) for b in range(BLOCKS)]
-        nc.sync.dma_start(states[0][:], rT[0:P, :])
         edge_weight = [keep.tile([P, HALF], F32, name="edge_weight%d" % h) for h in range(HALVES)]
+
+        def load_state(b):
+            nc.sync.dma_start(states[b][:], rT[b * P : (b + 1) * P, :])
+
+        load_floats(1)
+        load_state(0)
         nc.sync.dma_start(edge_weight[0][:], wgo[:, 0:HALF])
         load_codes(range(1, BLOCKS))
+        load_floats(2)
         nc.sync.dma_start(edge_weight[1][:], wgo[:, HALF:J])
-        nc.sync.dma_start(states[1][:], rT[P : 2 * P, :])
-        load_floats((2, 3))
-        for b in range(2, BLOCKS):
-            nc.sync.dma_start(states[b][:], rT[b * P : (b + 1) * P, :])
+        load_state(1)
+        load_floats(3)
+        load_state(2)
+        load_state(3)
 
         pick_words(0, "both0")
         quantize(0)
@@ -194,9 +211,9 @@ def tile_list_rgg_ownL_kernel(
             return bank[:, 0:count]
 
         def multiply(unit, gate):
-            count = unit[2]
-            if unit[0] not in made:
-                quantize(unit[0])
+            b, first, count = unit
+            if b not in made:
+                quantize(b)
             gate_sum = product("gate_sum", (("wb", SRC), ("wa", DST)), unit)
             nc.scalar.activation(gate[:, 0:count], gate_sum, SIGMOID)
             own_sum = product("own_sum", (("wo", DST),), unit)
@@ -209,8 +226,7 @@ def tile_list_rgg_ownL_kernel(
             nc.vector.tensor_tensor(gated[:, 0 : gate.shape[1]], message, gate, MULT)
             return gated, own
 
-        def turn(unit, gated, own):
-            count = unit[2]
+        def turn(count, gated, own):
             turned = psum.tile([P, HALF], F32, name="turned")
             for e in range(0, count, P):
                 cols = slice(e, e + P)
@@ -230,9 +246,8 @@ def tile_list_rgg_ownL_kernel(
         terms = let_through(keep.tile([P, HALF], F32, name="first_gated"), sums)
         clear_page()
         sums = multiply(units[1], fresh_gate())
-        for u, unit in enumerate(units):
-            b, first, count = unit
-            update = turn(unit, *terms)
+        for u, (b, first, count) in enumerate(units):
+            update = turn(count, *terms)
             total = ring.tile([P, HALF], F32, name="total")
             listed = offsets(DST, first, count)
             nc.vector.tensor_tensor(total[:, 0:count], states[b][:].indirect(listed), update[:, 0:count], ADD)

@@ -15,7 +15,7 @@ U8 = mybir.dt.uint8
 FP8X4 = mybir.dt.float8_e4m3fn_x4
 FP4X4 = mybir.dt.float4_e2m1fn_x4
 MULT = mybir.AluOpType.mult
-ADD = mybir.AluOpType.add
+COPY = mybir.ActivationFunctionType.Copy
 SIGMOID = mybir.ActivationFunctionType.Sigmoid
 
 P = 128
@@ -33,6 +33,8 @@ PAGES = 2
 MOVED_ROWS = 112
 DST, SRC = 0, 1
 SIDES = (DST, SRC)
+UNITS = BLOCKS * HALVES
+GROUPS = HALF // P
 
 
 def tile_list_rgg_ownL_kernel(
@@ -42,7 +44,8 @@ def tile_list_rgg_ownL_kernel(
     with ExitStack() as ctx:
         keep = ctx.enter_context(tc.tile_pool(name="keep", bufs=1))
         ring = ctx.enter_context(tc.tile_pool(name="ring", bufs=2))
-        psum = ctx.enter_context(tc.psum_pool(name="psum", bufs=2))
+        deep = ctx.enter_context(tc.tile_pool(name="deep", bufs=4))
+        psum = ctx.enter_context(tc.psum_pool(name="psum", bufs=1))
 
         dst_list = keep.tile([P, J // STRIPE], U16, name="dst_list")
         src_list = keep.tile([P, J // STRIPE], U16, name="src_list")
@@ -54,30 +57,23 @@ def tile_list_rgg_ownL_kernel(
         table_scales = keep.tile([P, T], U8, name="table_scales", align_bytes=64)
         nc.gpsimd.memset(table_scales[:].bitcast(I32), 0)
         planes = keep.tile([P, 2 * PASSES * N + len(SIDES) * J], U8, name="planes", align_bytes=64)
-        nc.vector.memset(planes[:].bitcast(I32), 0)
+        nc.gpsimd.memset(planes[:].bitcast(I32), 0)
         given_scales = planes[:, 0 : 2 * PASSES * N].rearrange("p (w a n) -> p w a n", w=2, a=PASSES)
         moved_scales = planes[:, 2 * PASSES * N :]
-
-        pages = []
-
-        def clear_page():
-            name = "page%d" % len(pages)
-            page = keep.tile([P, T], F32, name=name, tag=name)
-            nc.vector.memset(page[:].bitcast(I32), 0)
-            pages.append(page)
-
-        clear_page()
         ident = keep.tile([P, P], F32, name="ident")
         make_identity(nc, ident[:])
+        pages = [keep.tile([P, T], F32, name="page%d" % i) for i in range(PAGES)]
+        for page in pages:
+            nc.gpsimd.memset(page[:].bitcast(I32), 0)
 
         float_weights = (wb, wo)
         raw = {}
 
-        def load_floats(b):
-            for w, source in enumerate(float_weights):
+        def load_floats(b, which):
+            for w in which:
                 for a in range(PASSES):
                     t = keep.tile([P, PACK, P], F32, name="raw%d%d%d" % (w, b, a))
-                    rows = source[a * P * PACK : (a + 1) * P * PACK, b * P : (b + 1) * P]
+                    rows = float_weights[w][a * P * PACK : (a + 1) * P * PACK, b * P : (b + 1) * P]
                     nc.sync.dma_start(t[:], rows.rearrange("(p i) n -> p i n", i=PACK))
                     raw[w, b, a] = t
 
@@ -117,23 +113,26 @@ def tile_list_rgg_ownL_kernel(
                 nc.vector.tensor_copy(t[:].bitcast(U16), pairs.rearrange("p (j a) -> p a j", a=PASSES))
                 parted[side, h] = t
 
+        grouped = {}
         made = {}
+        shape = [P, len(float_weights), PASSES, P]
+
+        def cast(b, w):
+            if b not in grouped:
+                grouped[b] = keep.tile(shape + [PACK], BF16, name="grouped%d" % b, tag="stage%d" % b, align_bytes=64)
+            for a in range(PASSES):
+                nc.scalar.copy(
+                    grouped[b][:, w, a].rearrange("p (c m) i -> p c i m", m=LINE),
+                    raw[w, b, a][:].rearrange("p i (c m) -> p c i m", m=LINE),
+                )
 
         def quantize(b):
-            shape = [P, len(float_weights), PASSES, P]
-            grouped = keep.tile(shape + [PACK], BF16, name="grouped%d" % b, tag="stage%d" % b, align_bytes=64)
-            for w in range(len(float_weights)):
-                for a in range(PASSES):
-                    nc.scalar.copy(
-                        grouped[:, w, a].rearrange("p (c m) i -> p c i m", m=LINE),
-                        raw[w, b, a][:].rearrange("p i (c m) -> p c i m", m=LINE),
-                    )
             codes = keep.tile(shape, U32, name="codes%d" % b, align_bytes=64)
             scales = keep.tile(shape, U8, name="scales%d" % b, align_bytes=64)
             nc.vector.quantize_mx(
                 out=codes[:].rearrange("p w a n -> p (w a n)").bitcast(FP8X4),
                 scales=scales[:].rearrange("p w a n -> p (w a n)"),
-                in_=grouped[:].rearrange("p w a n i -> p (w a n i)"),
+                in_=grouped[b][:].rearrange("p w a n i -> p (w a n i)"),
             )
             made[b] = (codes, scales)
 
@@ -147,9 +146,12 @@ def tile_list_rgg_ownL_kernel(
         table_words = keep.tile([P, T], I32, name="table_words", align_bytes=64)
         nc.sync.dma_start(table_words[:], tab_words[0].rearrange("p t b -> p (t b)").bitcast(I32))
         load_scales(0, wa_scales)
-        load_floats(0)
+        load_floats(0, (0, 1))
         load_scales(1, wc_scales)
         load_codes(range(0, 1))
+        weight_rows = keep.tile([P, P], F32, name="weight_rows")
+        nc.sync.dma_start(weight_rows[:], wgo[0 : P * P // J, :].rearrange("r (e p) -> (r e) p", p=P))
+        load_floats(1, (0,))
 
         picked_scales = keep.tile([P, len(SIDES) * J], U8, name="picked_scales", align_bytes=64)
         for side in SIDES:
@@ -160,25 +162,32 @@ def tile_list_rgg_ownL_kernel(
         edge_scales = (picked_scales[:], moved_scales)
 
         states = [keep.tile([P, T], F32, name="state%d" % b) for b in range(BLOCKS)]
-        edge_weight = [keep.tile([P, HALF], F32, name="edge_weight%d" % h) for h in range(HALVES)]
 
         def load_state(b):
             nc.sync.dma_start(states[b][:], rT[b * P : (b + 1) * P, :])
 
-        load_floats(1)
+        load_floats(1, (1,))
         load_state(0)
-        nc.sync.dma_start(edge_weight[0][:], wgo[:, 0:HALF])
         load_codes(range(1, BLOCKS))
-        load_floats(2)
-        nc.sync.dma_start(edge_weight[1][:], wgo[:, HALF:J])
         load_state(1)
-        load_floats(3)
+        load_floats(2, (0, 1))
         load_state(2)
+        load_floats(3, (0, 1))
         load_state(3)
 
         pick_words(0, "both0")
+        cast(0, 0)
+        cast(0, 1)
         quantize(0)
         pick_words(1, "stage0")
+
+        def bank(kind, u):
+            return psum.tile([P, HALF], F32, name="bank", tag="%s%d" % (kind, u % 2))
+
+        turned_weights = bank("c", 1)
+        nc.tensor.transpose(turned_weights[:, 0:P], weight_rows[:], ident[:])
+        edge_weight = keep.tile([P, J // P], F32, name="edge_weight")
+        nc.scalar.copy(edge_weight[:], turned_weights[:, 0 : J // P])
 
         def weight(w, a, b):
             cols = slice(b * P, (b + 1) * P)
@@ -190,73 +199,97 @@ def tile_list_rgg_ownL_kernel(
             f = ("wb", "wo").index(w)
             return codes[:, f, a, :].bitcast(FP8X4), scales[:, f, a, :]
 
-        def product(name, terms, unit):
-            b, first, count = unit
-            bank = psum.tile([P, HALF], F32, name=name)
+        def product(acc, terms, u):
+            b, h = divmod(u, HALVES)
             steps = [(w, side, a) for w, side in terms for a in reversed(range(PASSES))]
-            for e in range(0, count, P):
-                h, j = divmod(first + e, HALF)
-                for s, (w, side, a) in enumerate(steps):
-                    codes, scales = weight(w, a, b)
-                    column = side * J + first + e
-                    nc.tensor.matmul_mx(
-                        out=bank[:, e : e + P],
-                        lhsT=parted[side, h][:, a, 2 * j : 2 * (j + P)].bitcast(FP4X4),
-                        lhsT_scale=edge_scales[a][:, column : column + P],
-                        rhs=codes,
-                        rhs_scale=scales,
-                        start=(s == 0),
-                        stop=(s == len(steps) - 1),
+            for s, (w, side, a) in enumerate(steps):
+                codes, scales = weight(w, a, b)
+                column = side * J + h * HALF
+                nc.tensor.matmul_mx(
+                    out=acc[:],
+                    lhsT=codes,
+                    lhsT_scale=scales,
+                    rhs=parted[side, h][:, a, :].bitcast(FP4X4),
+                    rhs_scale=edge_scales[a][:, column : column + HALF],
+                    start=(s == 0),
+                    stop=(s == len(steps) - 1),
+                )
+
+        residual = {}
+        gated = {}
+        own = {}
+        weighted = {}
+
+        def pick_state(u):
+            b, h = divmod(u, HALVES)
+            residual[u] = deep.tile([P, HALF], F32, name="residual")
+            nc.vector.tensor_copy(residual[u][:], states[b][:].indirect(offsets(DST, h * HALF, HALF)))
+
+        def make_message(u):
+            gate_sum = bank("a", u)
+            product(gate_sum, (("wb", SRC), ("wa", DST)), u)
+            gate = ring.tile([P, HALF], F32, name="gate")
+            nc.scalar.activation(gate[:], gate_sum[:], SIGMOID)
+            message_sum = bank("b", u)
+            product(message_sum, (("wc", SRC),), u)
+            message = ring.tile([P, HALF], F32, name="message")
+            nc.scalar.copy(message[:], message_sum[:])
+            gated[u] = ring.tile([P, HALF], F32, name="gated")
+            nc.gpsimd.tensor_tensor(gated[u][:], message[:], gate[:], MULT)
+
+        def make_own(u):
+            own_sum = bank("c", u)
+            product(own_sum, (("wo", DST),), u)
+            own[u] = ring.tile([P, HALF], F32, name="own")
+            nc.scalar.copy(own[u][:], own_sum[:])
+
+        def add_up(u, step):
+            total = bank("b", step)
+            terms = (gated[u], own[u], residual[u])
+            for e in range(GROUPS):
+                cols = slice(e * P, (e + 1) * P)
+                for s, term in enumerate(terms):
+                    nc.tensor.matmul(
+                        total[:, cols], lhsT=term[:, cols], rhs=ident[:], is_transpose=True,
+                        start=(s == 0), stop=(s == len(terms) - 1),
                     )
-            return bank[:, 0:count]
+            weighted[u] = ring.tile([P, HALF], F32, name="weighted")
+            for e in range(GROUPS):
+                cols = slice(e * P, (e + 1) * P)
+                g = (u % HALVES) * GROUPS + e
+                nc.scalar.activation(weighted[u][:, cols], total[:, cols], COPY, scale=edge_weight[:, g : g + 1])
 
-        def multiply(unit, gate):
-            b, first, count = unit
-            if b not in made:
-                quantize(b)
-            gate_sum = product("gate_sum", (("wb", SRC), ("wa", DST)), unit)
-            nc.scalar.activation(gate[:, 0:count], gate_sum, SIGMOID)
-            own_sum = product("own_sum", (("wo", DST),), unit)
-            own = ring.tile([P, HALF], F32, name="own")
-            nc.scalar.copy(own[:, 0:count], own_sum)
-            return product("message", (("wc", SRC),), unit), gate[:, 0:count], own
-
-        def let_through(gated, sums):
-            message, gate, own = sums
-            nc.vector.tensor_tensor(gated[:, 0 : gate.shape[1]], message, gate, MULT)
-            return gated, own
-
-        def turn(count, gated, own):
-            turned = psum.tile([P, HALF], F32, name="turned")
-            for e in range(0, count, P):
-                cols = slice(e, e + P)
-                nc.tensor.matmul(turned[:, cols], lhsT=gated[:, cols], rhs=ident[:], is_transpose=True, start=True, stop=False)
-                nc.tensor.matmul(turned[:, cols], lhsT=own[:, cols], rhs=ident[:], is_transpose=True, start=False, stop=True)
-            update = ring.tile([P, HALF], F32, name="update")
-            nc.scalar.copy(update[:, 0:count], turned[:, 0:count])
-            return update
-
-        def fresh_gate():
-            return ring.tile([P, HALF], F32, name="gate")
-
-        units = [(b, first, HALF) for b in range(BLOCKS) for first in range(0, J, HALF)]
-        units[0:1] = [(0, first, HALF // 2) for first in range(0, HALF, HALF // 2)]
-
-        sums = multiply(units[0], keep.tile([P, HALF], F32, name="first_gate", tag="page1"))
-        terms = let_through(keep.tile([P, HALF], F32, name="first_gated"), sums)
-        clear_page()
-        sums = multiply(units[1], fresh_gate())
-        for u, (b, first, count) in enumerate(units):
-            update = turn(count, *terms)
-            total = ring.tile([P, HALF], F32, name="total")
-            listed = offsets(DST, first, count)
-            nc.vector.tensor_tensor(total[:, 0:count], states[b][:].indirect(listed), update[:, 0:count], ADD)
-            if u + 1 < len(units):
-                terms = let_through(update, sums)
+        def put(u, step):
+            b, h = divmod(u, HALVES)
+            back = bank("a", step)
+            for e in range(GROUPS):
+                cols = slice(e * P, (e + 1) * P)
+                nc.tensor.transpose(back[:, cols], weighted[u][:, cols], ident[:])
+            result = deep.tile([P, HALF], F32, name="result")
+            nc.scalar.copy(result[:], back[:])
             page = pages[b % PAGES]
-            h, j = divmod(first, HALF)
-            nc.vector.tensor_tensor(page[:].indirect(listed), total[:, 0:count], edge_weight[h][:, j : j + count], MULT)
-            if first + count == J:
+            nc.vector.tensor_copy(page[:].indirect(offsets(DST, h * HALF, HALF)), result[:])
+            if h == HALVES - 1:
                 nc.sync.dma_start(out[b * P : (b + 1) * P, :], page[:])
-            if u + 2 < len(units):
-                sums = multiply(units[u + 2], fresh_gate())
+
+        cast(1, 0)
+        cast(1, 1)
+        quantize(1)
+        for u in range(4):
+            pick_state(u)
+        for step in range(UNITS + 2):
+            if step < UNITS:
+                make_message(step)
+            if step >= 2:
+                put(step - 2, step)
+            if step < UNITS:
+                make_own(step)
+            if 1 <= step <= UNITS:
+                add_up(step - 1, step)
+                if step + 3 < UNITS:
+                    pick_state(step + 3)
+            if 1 <= step <= 4:
+                b, w = divmod(step - 1, 2)
+                cast(b + 2, w)
+                if w == 1:
+                    quantize(b + 2)

@@ -16,6 +16,7 @@ FP8X4 = mybir.dt.float8_e4m3fn_x4
 FP4X4 = mybir.dt.float4_e2m1fn_x4
 MULT = mybir.AluOpType.mult
 COPY = mybir.ActivationFunctionType.Copy
+ADD = mybir.AluOpType.add
 SIGMOID = mybir.ActivationFunctionType.Sigmoid
 
 P = 128
@@ -35,6 +36,7 @@ DST, SRC = 0, 1
 SIDES = (DST, SRC)
 UNITS = BLOCKS * HALVES
 GROUPS = HALF // P
+BANKS = {"gate": 2, "message": 1, "own": 1, "total": 2, "back": 2}
 
 
 def tile_list_rgg_ownL_kernel(
@@ -102,12 +104,12 @@ def tile_list_rgg_ownL_kernel(
 
         def pick_words(h, tag):
             both = keep.tile([P, len(SIDES) * HALF], I32, name="both%d" % h, tag=tag, align_bytes=64)
-            for side in SIDES:
+            for side in (SRC, DST):
                 window = table_words[:].bitcast(U32)
                 nc.vector.tensor_copy(
                     both[:, side * HALF : (side + 1) * HALF].bitcast(U32), window.indirect(offsets(side, h * HALF, HALF))
                 )
-            for side in SIDES:
+            for side in (SRC, DST):
                 t = keep.tile([P, PASSES, 2 * HALF], U8, name="parted%d%d" % (side, h), align_bytes=64)
                 pairs = both[:, side * HALF : (side + 1) * HALF].bitcast(U16)
                 nc.vector.tensor_copy(t[:].bitcast(U16), pairs.rearrange("p (j a) -> p a j", a=PASSES))
@@ -151,7 +153,12 @@ def tile_list_rgg_ownL_kernel(
         load_codes(range(0, 1))
         weight_rows = keep.tile([P, P], F32, name="weight_rows")
         nc.sync.dma_start(weight_rows[:], wgo[0 : P * P // J, :].rearrange("r (e p) -> (r e) p", p=P))
-        load_floats(1, (0,))
+        states = [keep.tile([P, T], F32, name="state%d" % b) for b in range(BLOCKS)]
+
+        def load_state(b):
+            nc.sync.dma_start(states[b][:], rT[b * P : (b + 1) * P, :])
+
+        load_state(0)
 
         picked_scales = keep.tile([P, len(SIDES) * J], U8, name="picked_scales", align_bytes=64)
         for side in SIDES:
@@ -161,16 +168,11 @@ def tile_list_rgg_ownL_kernel(
         )
         edge_scales = (picked_scales[:], moved_scales)
 
-        states = [keep.tile([P, T], F32, name="state%d" % b) for b in range(BLOCKS)]
-
-        def load_state(b):
-            nc.sync.dma_start(states[b][:], rT[b * P : (b + 1) * P, :])
-
-        load_floats(1, (1,))
-        load_state(0)
-        load_codes(range(1, BLOCKS))
+        load_floats(1, (0, 1))
+        load_codes(range(1, 2))
         load_state(1)
         load_floats(2, (0, 1))
+        load_codes(range(2, BLOCKS))
         load_state(2)
         load_floats(3, (0, 1))
         load_state(3)
@@ -182,12 +184,21 @@ def tile_list_rgg_ownL_kernel(
         pick_words(1, "stage0")
 
         def bank(kind, u):
-            return psum.tile([P, HALF], F32, name="bank", tag="%s%d" % (kind, u % 2))
+            return psum.tile([P, HALF], F32, name="bank", tag="%s%d" % (kind, u % BANKS[kind]))
 
-        turned_weights = bank("c", 1)
+        turned_weights = bank("back", 1)
         nc.tensor.transpose(turned_weights[:, 0:P], weight_rows[:], ident[:])
         edge_weight = keep.tile([P, J // P], F32, name="edge_weight")
         nc.scalar.copy(edge_weight[:], turned_weights[:, 0 : J // P])
+
+        spread_weight = {}
+        for h in range(1, HALVES):
+            spread = bank("total", h)
+            for e in range(GROUPS):
+                g = h * GROUPS + e
+                nc.tensor.transpose(spread[:, e * P : (e + 1) * P], edge_weight[:, g : g + 1].to_broadcast([P, P]), ident[:])
+            spread_weight[h] = keep.tile([P, HALF], F32, name="spread_weight%d" % h)
+            nc.scalar.copy(spread_weight[h][:], spread[:])
 
         def weight(w, a, b):
             cols = slice(b * P, (b + 1) * P)
@@ -216,36 +227,42 @@ def tile_list_rgg_ownL_kernel(
                 )
 
         residual = {}
+        gate = {}
+        message = {}
         gated = {}
         own = {}
         weighted = {}
 
-        def pick_state(u):
+        def pick_state(u, target):
             b, h = divmod(u, HALVES)
-            residual[u] = deep.tile([P, HALF], F32, name="residual")
-            nc.vector.tensor_copy(residual[u][:], states[b][:].indirect(offsets(DST, h * HALF, HALF)))
+            residual[u] = target
+            nc.vector.tensor_copy(target, states[b][:].indirect(offsets(DST, h * HALF, HALF)))
+
+        def make_gate(u, terms):
+            gate_sum = bank("gate", u)
+            product(gate_sum, terms, u)
+            gate[u] = ring.tile([P, HALF], F32, name="gate")
+            nc.scalar.activation(gate[u][:], gate_sum[:], SIGMOID)
 
         def make_message(u):
-            gate_sum = bank("a", u)
-            product(gate_sum, (("wb", SRC), ("wa", DST)), u)
-            gate = ring.tile([P, HALF], F32, name="gate")
-            nc.scalar.activation(gate[:], gate_sum[:], SIGMOID)
-            message_sum = bank("b", u)
+            message_sum = bank("message", u)
             product(message_sum, (("wc", SRC),), u)
-            message = ring.tile([P, HALF], F32, name="message")
-            nc.scalar.copy(message[:], message_sum[:])
-            gated[u] = ring.tile([P, HALF], F32, name="gated")
-            nc.gpsimd.tensor_tensor(gated[u][:], message[:], gate[:], MULT)
+            message[u] = ring.tile([P, HALF], F32, name="message")
+            nc.scalar.copy(message[u][:], message_sum[:])
+
+        def let_through(u, target):
+            gated[u] = target
+            nc.gpsimd.tensor_tensor(target, message[u][:], gate[u][:], MULT)
 
         def make_own(u):
-            own_sum = bank("c", u)
+            own_sum = bank("own", u)
             product(own_sum, (("wo", DST),), u)
             own[u] = ring.tile([P, HALF], F32, name="own")
             nc.scalar.copy(own[u][:], own_sum[:])
 
-        def add_up(u, step):
-            total = bank("b", step)
-            terms = (gated[u], own[u], residual[u])
+        def add_up(u):
+            total = bank("total", u)
+            terms = (gated[u], own[u][:], residual[u])
             for e in range(GROUPS):
                 cols = slice(e * P, (e + 1) * P)
                 for s, term in enumerate(terms):
@@ -259,37 +276,64 @@ def tile_list_rgg_ownL_kernel(
                 g = (u % HALVES) * GROUPS + e
                 nc.scalar.activation(weighted[u][:, cols], total[:, cols], COPY, scale=edge_weight[:, g : g + 1])
 
-        def put(u, step):
-            b, h = divmod(u, HALVES)
-            back = bank("a", step)
+        def turn_back(u):
+            back = bank("back", u)
             for e in range(GROUPS):
                 cols = slice(e * P, (e + 1) * P)
                 nc.tensor.transpose(back[:, cols], weighted[u][:, cols], ident[:])
             result = deep.tile([P, HALF], F32, name="result")
             nc.scalar.copy(result[:], back[:])
+            return result
+
+        def finish_on_gpsimd(u, first, second, third):
+            partial = ring.tile([P, HALF], F32, name="partial")
+            nc.gpsimd.tensor_tensor(partial[:], first, second, ADD)
+            total = ring.tile([P, HALF], F32, name="partial")
+            nc.gpsimd.tensor_tensor(total[:], partial[:], third, ADD)
+            result = deep.tile([P, HALF], F32, name="result")
+            nc.gpsimd.tensor_tensor(result[:], total[:], spread_weight[u % HALVES][:], MULT)
+            return result
+
+        def put(u, result):
+            b, h = divmod(u, HALVES)
             page = pages[b % PAGES]
             nc.vector.tensor_copy(page[:].indirect(offsets(DST, h * HALF, HALF)), result[:])
             if h == HALVES - 1:
                 nc.sync.dma_start(out[b * P : (b + 1) * P, :], page[:])
 
+        def fresh(pool, name):
+            return pool.tile([P, HALF], F32, name=name)[:]
+
+        pick_state(0, fresh(deep, "residual"))
+        pick_state(1, fresh(deep, "residual"))
+        make_message(0)
+        make_gate(0, (("wa", DST), ("wb", SRC)))
+        make_own(0)
         cast(1, 0)
         cast(1, 1)
         quantize(1)
-        for u in range(4):
-            pick_state(u)
-        for step in range(UNITS + 2):
-            if step < UNITS:
-                make_message(step)
-            if step >= 2:
-                put(step - 2, step)
-            if step < UNITS:
+        pick_state(2, fresh(deep, "residual"))
+        pick_state(3, fresh(deep, "residual"))
+        let_through(0, keep.tile([P, HALF], F32, name="gated0", tag="stage0", align_bytes=64)[:])
+        last = UNITS - 1
+        for step in range(1, UNITS):
+            if step == last:
                 make_own(step)
-            if 1 <= step <= UNITS:
-                add_up(step - 1, step)
-                if step + 3 < UNITS:
-                    pick_state(step + 3)
-            if 1 <= step <= 4:
+            make_gate(step, (("wb", SRC), ("wa", DST)))
+            make_message(step)
+            if step == 1:
+                let_through(step, keep.tile([P, HALF], F32, name="gated1", tag="stage1", align_bytes=64)[:])
+            else:
+                let_through(step, fresh(ring, "gated"))
+            add_up(step - 1)
+            if step + 3 < UNITS:
+                pick_state(step + 3, fresh(deep, "residual"))
+            if step < last:
+                make_own(step)
+            put(step - 1, turn_back(step - 1))
+            if step <= 4:
                 b, w = divmod(step - 1, 2)
                 cast(b + 2, w)
                 if w == 1:
                     quantize(b + 2)
+        put(last, finish_on_gpsimd(last, own[last][:], residual[last], gated[last]))

@@ -59,14 +59,13 @@ def tile_list_rgg_ownL_kernel(
         table_scales = keep.tile([P, T], U8, name="table_scales", align_bytes=64)
         nc.gpsimd.memset(table_scales[:].bitcast(I32), 0)
         planes = keep.tile([P, 2 * PASSES * N + len(SIDES) * J], U8, name="planes", align_bytes=64)
-        nc.gpsimd.memset(planes[:].bitcast(I32), 0)
+        nc.vector.memset(planes[:].bitcast(I32), 0)
         given_scales = planes[:, 0 : 2 * PASSES * N].rearrange("p (w a n) -> p w a n", w=2, a=PASSES)
         moved_scales = planes[:, 2 * PASSES * N :]
         ident = keep.tile([P, P], F32, name="ident")
         make_identity(nc, ident[:])
-        pages = [keep.tile([P, T], F32, name="page%d" % i) for i in range(PAGES)]
-        for page in pages:
-            nc.gpsimd.memset(page[:].bitcast(I32), 0)
+        pages = [keep.tile([P, T], F32, name="page0")]
+        nc.vector.memset(pages[0][:].bitcast(I32), 0)
 
         float_weights = (wb, wo)
         raw = {}
@@ -270,7 +269,10 @@ def tile_list_rgg_ownL_kernel(
                         total[:, cols], lhsT=term[:, cols], rhs=ident[:], is_transpose=True,
                         start=(s == 0), stop=(s == len(terms) - 1),
                     )
-            weighted[u] = ring.tile([P, HALF], F32, name="weighted")
+            if u == 0:
+                weighted[u] = keep.tile([P, HALF], F32, name="weighted0", tag="page1")
+            else:
+                weighted[u] = ring.tile([P, HALF], F32, name="weighted")
             for e in range(GROUPS):
                 cols = slice(e * P, (e + 1) * P)
                 g = (u % HALVES) * GROUPS + e
@@ -331,6 +333,9 @@ def tile_list_rgg_ownL_kernel(
             if step < last:
                 make_own(step)
             put(step - 1, turn_back(step - 1))
+            if step == 1:
+                pages.append(keep.tile([P, T], F32, name="page1", tag="page1"))
+                nc.gpsimd.memset(pages[1][:].bitcast(I32), 0)
             if step <= 4:
                 b, w = divmod(step - 1, 2)
                 cast(b + 2, w)

@@ -64,6 +64,8 @@ def tile_list_rgg_ownL_kernel(
         moved_scales = planes[:, 2 * PASSES * N :]
         ident = keep.tile([P, P], F32, name="ident")
         make_identity(nc, ident[:])
+        warm = keep.tile([P, 1], F32, name="warm")
+        nc.scalar.activation(warm[:], ident[:, 0:1], SIGMOID)
         pages = [keep.tile([P, T], F32, name="page0")]
         nc.vector.memset(pages[0][:].bitcast(I32), 0)
 

@@ -59,15 +59,17 @@ def tile_list_rgg_ownL_kernel(
         table_scales = keep.tile([P, T], U8, name="table_scales", align_bytes=64)
         nc.gpsimd.memset(table_scales[:].bitcast(I32), 0)
         planes = keep.tile([P, 2 * PASSES * N + len(SIDES) * J], U8, name="planes", align_bytes=64)
-        nc.vector.memset(planes[:].bitcast(I32), 0)
+        nc.gpsimd.memset(planes[:].bitcast(I32), 0)
         given_scales = planes[:, 0 : 2 * PASSES * N].rearrange("p (w a n) -> p w a n", w=2, a=PASSES)
         moved_scales = planes[:, 2 * PASSES * N :]
         ident = keep.tile([P, P], F32, name="ident")
         make_identity(nc, ident[:])
-        warm = keep.tile([P, 1], F32, name="warm")
-        nc.scalar.activation(warm[:], ident[:, 0:1], SIGMOID)
-        pages = [keep.tile([P, T], F32, name="page0")]
-        nc.vector.memset(pages[0][:].bitcast(I32), 0)
+        warm = keep.tile([P, 2], F32, name="warm")
+        nc.vector.memset(warm[:, 0:1], 0.0)
+        nc.scalar.activation(warm[:, 1:2], warm[:, 0:1], SIGMOID)
+        pages = [keep.tile([P, T], F32, name="page%d" % i) for i in range(PAGES)]
+        for page in pages:
+            nc.gpsimd.memset(page[:].bitcast(I32), 0)
 
         float_weights = (wb, wo)
         raw = {}
@@ -251,9 +253,9 @@ def tile_list_rgg_ownL_kernel(
             message[u] = ring.tile([P, HALF], F32, name="message")
             nc.scalar.copy(message[u][:], message_sum[:])
 
-        def let_through(u, target):
+        def let_through(u, target, cols=slice(0, HALF)):
             gated[u] = target
-            nc.gpsimd.tensor_tensor(target, message[u][:], gate[u][:], MULT)
+            nc.gpsimd.tensor_tensor(target[:, cols], message[u][:, cols], gate[u][:, cols], MULT)
 
         def make_own(u):
             own_sum = bank("own", u)
@@ -261,32 +263,30 @@ def tile_list_rgg_ownL_kernel(
             own[u] = ring.tile([P, HALF], F32, name="own")
             nc.scalar.copy(own[u][:], own_sum[:])
 
-        def add_up(u):
-            total = bank("total", u)
+        def add_up(u, groups=range(GROUPS)):
+            total = bank("total", u + groups[0] // 2)
             terms = (gated[u], own[u][:], residual[u])
-            for e in range(GROUPS):
+            for e in groups:
                 cols = slice(e * P, (e + 1) * P)
                 for s, term in enumerate(terms):
                     nc.tensor.matmul(
                         total[:, cols], lhsT=term[:, cols], rhs=ident[:], is_transpose=True,
                         start=(s == 0), stop=(s == len(terms) - 1),
                     )
-            if u == 0:
-                weighted[u] = keep.tile([P, HALF], F32, name="weighted0", tag="page1")
-            else:
-                weighted[u] = ring.tile([P, HALF], F32, name="weighted")
-            for e in range(GROUPS):
+            weighted[u, groups[0]] = ring.tile([P, HALF], F32, name="weighted")
+            for e in groups:
                 cols = slice(e * P, (e + 1) * P)
                 g = (u % HALVES) * GROUPS + e
-                nc.scalar.activation(weighted[u][:, cols], total[:, cols], COPY, scale=edge_weight[:, g : g + 1])
+                nc.scalar.activation(weighted[u, groups[0]][:, cols], total[:, cols], COPY, scale=edge_weight[:, g : g + 1])
 
-        def turn_back(u):
-            back = bank("back", u)
-            for e in range(GROUPS):
+        def turn_back(u, groups=range(GROUPS)):
+            back = bank("back", u + groups[0] // 2)
+            for e in groups:
                 cols = slice(e * P, (e + 1) * P)
-                nc.tensor.transpose(back[:, cols], weighted[u][:, cols], ident[:])
+                nc.tensor.transpose(back[:, cols], weighted[u, groups[0]][:, cols], ident[:])
             result = deep.tile([P, HALF], F32, name="result")
-            nc.scalar.copy(result[:], back[:])
+            cols = slice(groups[0] * P, (groups[-1] + 1) * P)
+            nc.scalar.copy(result[:, cols], back[:, cols])
             return result
 
         def finish_on_gpsimd(u, first, second, third):
@@ -298,10 +298,10 @@ def tile_list_rgg_ownL_kernel(
             nc.gpsimd.tensor_tensor(result[:], total[:], spread_weight[u % HALVES][:], MULT)
             return result
 
-        def put(u, result):
+        def put(u, result, first=0, count=HALF):
             b, h = divmod(u, HALVES)
             page = pages[b % PAGES]
-            nc.vector.tensor_copy(page[:].indirect(offsets(DST, h * HALF, HALF)), result[:])
+            nc.vector.tensor_copy(page[:].indirect(offsets(DST, h * HALF + first, count)), result[:, first : first + count])
             if h == HALVES - 1:
                 nc.sync.dma_start(out[b * P : (b + 1) * P, :], page[:])
 
@@ -318,7 +318,9 @@ def tile_list_rgg_ownL_kernel(
         quantize(1)
         pick_state(2, fresh(deep, "residual"))
         pick_state(3, fresh(deep, "residual"))
-        let_through(0, keep.tile([P, HALF], F32, name="gated0", tag="stage0", align_bytes=64)[:])
+        gated0 = keep.tile([P, HALF], F32, name="gated0", tag="stage0", align_bytes=64)[:]
+        for first in range(0, HALF, HALF // 2):
+            let_through(0, gated0, slice(first, first + HALF // 2))
         last = UNITS - 1
         for step in range(1, UNITS):
             if step == last:
@@ -329,15 +331,20 @@ def tile_list_rgg_ownL_kernel(
                 let_through(step, keep.tile([P, HALF], F32, name="gated1", tag="stage1", align_bytes=64)[:])
             else:
                 let_through(step, fresh(ring, "gated"))
-            add_up(step - 1)
+            if step == 1:
+                add_up(0, range(0, 2))
+                add_up(0, range(2, 4))
+            else:
+                add_up(step - 1)
             if step + 3 < UNITS:
                 pick_state(step + 3, fresh(deep, "residual"))
             if step < last:
                 make_own(step)
-            put(step - 1, turn_back(step - 1))
             if step == 1:
-                pages.append(keep.tile([P, T], F32, name="page1", tag="page1"))
-                nc.gpsimd.memset(pages[1][:].bitcast(I32), 0)
+                put(0, turn_back(0, range(0, 2)), 0, HALF // 2)
+                put(0, turn_back(0, range(2, 4)), HALF // 2, HALF // 2)
+            else:
+                put(step - 1, turn_back(step - 1))
             if step <= 4:
                 b, w = divmod(step - 1, 2)
                 cast(b + 2, w)

@@ -36,6 +36,7 @@ DST, SRC = 0, 1
 SIDES = (DST, SRC)
 UNITS = BLOCKS * HALVES
 GROUPS = HALF // P
+ON_GPSIMD = (5, 7)
 BANKS = {"gate": 2, "message": 1, "own": 1, "total": 2, "back": 2}
 
 
@@ -289,13 +290,16 @@ def tile_list_rgg_ownL_kernel(
             nc.scalar.copy(result[:, cols], back[:, cols])
             return result
 
-        def finish_on_gpsimd(u, first, second, third):
+        def add_on_gpsimd(u):
             partial = ring.tile([P, HALF], F32, name="partial")
-            nc.gpsimd.tensor_tensor(partial[:], first, second, ADD)
+            nc.gpsimd.tensor_tensor(partial[:], own[u][:], residual[u], ADD)
             total = ring.tile([P, HALF], F32, name="partial")
-            nc.gpsimd.tensor_tensor(total[:], partial[:], third, ADD)
+            nc.gpsimd.tensor_tensor(total[:], partial[:], gated[u], ADD)
+            return total
+
+        def weigh_on_gpsimd(total):
             result = deep.tile([P, HALF], F32, name="result")
-            nc.gpsimd.tensor_tensor(result[:], total[:], spread_weight[u % HALVES][:], MULT)
+            nc.gpsimd.tensor_tensor(result[:], total[:], spread_weight[1][:], MULT)
             return result
 
         def put(u, result, first=0, count=HALF):
@@ -323,7 +327,7 @@ def tile_list_rgg_ownL_kernel(
             let_through(0, gated0, slice(first, first + HALF // 2))
         last = UNITS - 1
         for step in range(1, UNITS):
-            if step == last:
+            if step in ON_GPSIMD:
                 make_own(step)
             make_gate(step, (("wb", SRC), ("wa", DST)))
             make_message(step)
@@ -334,20 +338,24 @@ def tile_list_rgg_ownL_kernel(
             if step == 1:
                 add_up(0, range(0, 2))
                 add_up(0, range(2, 4))
-            else:
+            elif step - 1 not in ON_GPSIMD:
                 add_up(step - 1)
             if step + 3 < UNITS:
                 pick_state(step + 3, fresh(deep, "residual"))
-            if step < last:
+            if step not in ON_GPSIMD:
                 make_own(step)
             if step == 1:
                 put(0, turn_back(0, range(0, 2)), 0, HALF // 2)
                 put(0, turn_back(0, range(2, 4)), HALF // 2, HALF // 2)
-            else:
+            elif step - 1 not in ON_GPSIMD:
                 put(step - 1, turn_back(step - 1))
+            if step in ON_GPSIMD and step < last:
+                put(step, weigh_on_gpsimd(add_on_gpsimd(step)))
             if step <= 4:
                 b, w = divmod(step - 1, 2)
                 cast(b + 2, w)
                 if w == 1:
                     quantize(b + 2)
-        put(last, finish_on_gpsimd(last, own[last][:], residual[last], gated[last]))
+        page = pages[(BLOCKS - 1) % PAGES]
+        nc.vector.tensor_tensor(page[:].indirect(offsets(DST, HALF, HALF)), add_on_gpsimd(last)[:], spread_weight[1][:], MULT)
+        nc.sync.dma_start(out[(BLOCKS - 1) * P : BLOCKS * P, :], page[:])

@@ -31,6 +31,7 @@ HALF = 512
 HALVES = J // HALF
 BLOCKS = N // P
 PAGES = 2
+SHIFT = QUAD // PASSES
 MOVED_ROWS = 112
 DST, SRC = 0, 1
 SIDES = (DST, SRC)
@@ -78,7 +79,8 @@ def tile_list_rgg_ownL_kernel(
         def load_floats(b, which):
             for w in which:
                 for a in range(PASSES):
-                    t = keep.tile([P, PACK, P], F32, name="raw%d%d%d" % (w, b, a))
+                    name = "raw%d%d%d" % (w, b, a)
+                    t = keep.tile([P, PACK, P], F32, name=name, tag=name, align_bytes=64)
                     rows = float_weights[w][a * P * PACK : (a + 1) * P * PACK, b * P : (b + 1) * P]
                     nc.sync.dma_start(t[:], rows.rearrange("(p i) n -> p i n", i=PACK))
                     raw[w, b, a] = t
@@ -143,12 +145,12 @@ def tile_list_rgg_ownL_kernel(
             made[b] = (codes, scales)
 
         nc.sync.dma_start(dst_list[:], offs2)
-        nc.sync.dma_start(src_list[:], offs)
-        for q in range(QUADS):
+        for r in range(ROWS):
             nc.sync.dma_start(
-                table_scales[QUAD * q : QUAD * q + PASSES * ROWS, :].bitcast(I32),
-                tab_scales[:, ROWS * q : ROWS * (q + 1), :].bitcast(I32),
+                table_scales[r : P : SHIFT, :].bitcast(I32),
+                tab_scales.rearrange("a (q r) t -> r q a t", r=ROWS)[r].bitcast(I32),
             )
+        nc.sync.dma_start(src_list[:], offs)
         table_words = keep.tile([P, T], I32, name="table_words", align_bytes=64)
         nc.sync.dma_start(table_words[:], tab_words[0].rearrange("p t b -> p (t b)").bitcast(I32))
         load_scales(0, wa_scales)
@@ -168,7 +170,7 @@ def tile_list_rgg_ownL_kernel(
         for side in SIDES:
             nc.vector.tensor_copy(picked_scales[:, side * J : (side + 1) * J], table_scales[:].indirect(lists[side][:]))
         nc.sync.dma_start(
-            moved_scales[0:MOVED_ROWS, :].bitcast(I32), picked_scales[ROWS : ROWS + MOVED_ROWS, :].bitcast(I32)
+            moved_scales[0:MOVED_ROWS, :].bitcast(I32), picked_scales[SHIFT : SHIFT + MOVED_ROWS, :].bitcast(I32)
         )
         edge_scales = (picked_scales[:], moved_scales)
 
@@ -185,7 +187,7 @@ def tile_list_rgg_ownL_kernel(
         cast(0, 0)
         cast(0, 1)
         quantize(0)
-        pick_words(1, "stage0")
+        pick_words(1, "raw101")
 
         def bank(kind, u):
             return psum.tile([P, HALF], F32, name="bank", tag="%s%d" % (kind, u % BANKS[kind]))
@@ -242,6 +244,19 @@ def tile_list_rgg_ownL_kernel(
             residual[u] = target
             nc.vector.tensor_copy(target, states[b][:].indirect(offsets(DST, h * HALF, HALF)))
 
+        def pick_block_state(b):
+            whole = keep.tile([P, J], F32, name="residual_block%d" % b)
+            nc.vector.tensor_copy(whole[:], states[b][:].indirect(dst_list[:]))
+            for h in range(HALVES):
+                residual[b * HALVES + h] = whole[:, h * HALF : (h + 1) * HALF]
+
+        whole_result = keep.tile([P, J], F32, name="whole_result")
+
+        def result_tile(u):
+            if u in (4, 5):
+                return whole_result[:, (u - 4) * HALF : (u - 3) * HALF]
+            return deep.tile([P, HALF], F32, name="result")
+
         def make_gate(u, terms):
             gate_sum = bank("gate", u)
             product(gate_sum, terms, u)
@@ -285,7 +300,7 @@ def tile_list_rgg_ownL_kernel(
             for e in groups:
                 cols = slice(e * P, (e + 1) * P)
                 nc.tensor.transpose(back[:, cols], weighted[u, groups[0]][:, cols], ident[:])
-            result = deep.tile([P, HALF], F32, name="result")
+            result = result_tile(u)
             cols = slice(groups[0] * P, (groups[-1] + 1) * P)
             nc.scalar.copy(result[:, cols], back[:, cols])
             return result
@@ -297,15 +312,18 @@ def tile_list_rgg_ownL_kernel(
             nc.gpsimd.tensor_tensor(total[:], partial[:], gated[u], ADD)
             return total
 
-        def weigh_on_gpsimd(total):
-            result = deep.tile([P, HALF], F32, name="result")
+        def weigh_on_gpsimd(u, total):
+            result = result_tile(u)
             nc.gpsimd.tensor_tensor(result[:], total[:], spread_weight[1][:], MULT)
             return result
 
         def put(u, result, first=0, count=HALF):
             b, h = divmod(u, HALVES)
             page = pages[b % PAGES]
-            nc.vector.tensor_copy(page[:].indirect(offsets(DST, h * HALF + first, count)), result[:, first : first + count])
+            if u == 5:
+                nc.vector.tensor_copy(page[:].indirect(dst_list[:]), whole_result[:])
+            elif u != 4:
+                nc.vector.tensor_copy(page[:].indirect(offsets(DST, h * HALF + first, count)), result[:, first : first + count])
             if h == HALVES - 1:
                 nc.sync.dma_start(out[b * P : (b + 1) * P, :], page[:])
 
@@ -322,7 +340,7 @@ def tile_list_rgg_ownL_kernel(
         quantize(1)
         pick_state(2, fresh(deep, "residual"))
         pick_state(3, fresh(deep, "residual"))
-        gated0 = keep.tile([P, HALF], F32, name="gated0", tag="stage0", align_bytes=64)[:]
+        gated0 = keep.tile([P, HALF], F32, name="gated0", tag="raw101", align_bytes=64)[:]
         for first in range(0, HALF, HALF // 2):
             let_through(0, gated0, slice(first, first + HALF // 2))
         last = UNITS - 1
@@ -340,8 +358,8 @@ def tile_list_rgg_ownL_kernel(
                 add_up(0, range(2, 4))
             elif step - 1 not in ON_GPSIMD:
                 add_up(step - 1)
-            if step + 3 < UNITS:
-                pick_state(step + 3, fresh(deep, "residual"))
+            if step in (1, 3):
+                pick_block_state(step // 2 + 2)
             if step not in ON_GPSIMD:
                 make_own(step)
             if step == 1:
@@ -350,7 +368,7 @@ def tile_list_rgg_ownL_kernel(
             elif step - 1 not in ON_GPSIMD:
                 put(step - 1, turn_back(step - 1))
             if step in ON_GPSIMD and step < last:
-                put(step, weigh_on_gpsimd(add_on_gpsimd(step)))
+                put(step, weigh_on_gpsimd(step, add_on_gpsimd(step)))
             if step <= 4:
                 b, w = divmod(step - 1, 2)
                 cast(b + 2, w)

@@ -38,6 +38,7 @@ SIDES = (DST, SRC)
 UNITS = BLOCKS * HALVES
 GROUPS = HALF // P
 ON_GPSIMD = (5, 7)
+WB, WO = 0, 1
 BANKS = {"gate": 2, "message": 1, "own": 1, "total": 2, "back": 2}
 
 
@@ -76,14 +77,14 @@ def tile_list_rgg_ownL_kernel(
         float_weights = (wb, wo)
         raw = {}
 
-        def load_floats(b, which):
-            for w in which:
-                for a in range(PASSES):
-                    name = "raw%d%d%d" % (w, b, a)
-                    t = keep.tile([P, PACK, P], F32, name=name, tag=name, align_bytes=64)
-                    rows = float_weights[w][a * P * PACK : (a + 1) * P * PACK, b * P : (b + 1) * P]
-                    nc.sync.dma_start(t[:], rows.rearrange("(p i) n -> p i n", i=PACK))
-                    raw[w, b, a] = t
+        def load_floats(w, blocks):
+            for a in range(PASSES):
+                name = "raw%d%d%d" % (w, blocks[0], a)
+                t = keep.tile([P, PACK, len(blocks) * P], F32, name=name, tag=name, align_bytes=64)
+                rows = float_weights[w][a * P * PACK : (a + 1) * P * PACK, blocks[0] * P : (blocks[-1] + 1) * P]
+                nc.sync.dma_start(t[:], rows.rearrange("(p i) n -> p i n", i=PACK))
+                for b in blocks:
+                    raw[w, b, a] = t[:, :, (b - blocks[0]) * P :]
 
         def load_scales(w, scales):
             for q in range(QUADS):
@@ -115,34 +116,39 @@ def tile_list_rgg_ownL_kernel(
                 nc.vector.tensor_copy(
                     both[:, side * HALF : (side + 1) * HALF].bitcast(U32), window.indirect(offsets(side, h * HALF, HALF))
                 )
+            return both
+
+        def part_words(both, h, tag):
+            t = keep.tile([P, len(SIDES), PASSES, 2 * HALF], U8, name="parted%d" % h, tag=tag, align_bytes=64)
             for side in (SRC, DST):
-                t = keep.tile([P, PASSES, 2 * HALF], U8, name="parted%d%d" % (side, h), align_bytes=64)
                 pairs = both[:, side * HALF : (side + 1) * HALF].bitcast(U16)
-                nc.vector.tensor_copy(t[:].bitcast(U16), pairs.rearrange("p (j a) -> p a j", a=PASSES))
-                parted[side, h] = t
+                nc.vector.tensor_copy(t[:, side].bitcast(U16), pairs.rearrange("p (j a) -> p a j", a=PASSES))
+                parted[side, h] = t[:, side]
 
         grouped = {}
         made = {}
-        shape = [P, len(float_weights), PASSES, P]
 
-        def cast(b, w):
-            if b not in grouped:
-                grouped[b] = keep.tile(shape + [PACK], BF16, name="grouped%d" % b, tag="stage%d" % b, align_bytes=64)
+        def cast(w, blocks):
+            name = "stage%d%d" % (w, blocks[0])
+            width = len(blocks) * P
+            grouped[w, blocks] = keep.tile([P, PASSES, width, PACK], BF16, name=name, tag=name, align_bytes=64)
             for a in range(PASSES):
                 nc.scalar.copy(
-                    grouped[b][:, w, a].rearrange("p (c m) i -> p c i m", m=LINE),
-                    raw[w, b, a][:].rearrange("p i (c m) -> p c i m", m=LINE),
+                    grouped[w, blocks][:, a].rearrange("p (c m) i -> p c i m", m=LINE),
+                    raw[w, blocks[0], a][:, :, 0:width].rearrange("p i (c m) -> p c i m", m=LINE),
                 )
 
-        def quantize(b):
-            codes = keep.tile(shape, U32, name="codes%d" % b, align_bytes=64)
-            scales = keep.tile(shape, U8, name="scales%d" % b, align_bytes=64)
+        def quantize(w, blocks):
+            shape = [P, PASSES, len(blocks) * P]
+            codes = keep.tile(shape, U32, name="codes%d%d" % (w, blocks[0]), align_bytes=64)
+            scales = keep.tile(shape, U8, name="scales%d%d" % (w, blocks[0]), align_bytes=64)
             nc.vector.quantize_mx(
-                out=codes[:].rearrange("p w a n -> p (w a n)").bitcast(FP8X4),
-                scales=scales[:].rearrange("p w a n -> p (w a n)"),
-                in_=grouped[b][:].rearrange("p w a n i -> p (w a n i)"),
+                out=codes[:].rearrange("p a n -> p (a n)").bitcast(FP8X4),
+                scales=scales[:].rearrange("p a n -> p (a n)"),
+                in_=grouped[w, blocks][:].rearrange("p a n i -> p (a n i)"),
             )
-            made[b] = (codes, scales)
+            for i, b in enumerate(blocks):
+                made[w, b] = (codes[:, :, i * P : (i + 1) * P], scales[:, :, i * P : (i + 1) * P])
 
         nc.sync.dma_start(dst_list[:], offs2)
         for r in range(ROWS):
@@ -153,18 +159,14 @@ def tile_list_rgg_ownL_kernel(
         nc.sync.dma_start(src_list[:], offs)
         table_words = keep.tile([P, T], I32, name="table_words", align_bytes=64)
         nc.sync.dma_start(table_words[:], tab_words[0].rearrange("p t b -> p (t b)").bitcast(I32))
-        load_scales(0, wa_scales)
-        load_floats(0, (0, 1))
         load_scales(1, wc_scales)
+        load_floats(WB, range(BLOCKS))
         load_codes(range(0, 1))
-        weight_rows = keep.tile([P, P], F32, name="weight_rows")
-        nc.sync.dma_start(weight_rows[:], wgo[0 : P * P // J, :].rearrange("r (e p) -> (r e) p", p=P))
+        load_scales(0, wa_scales)
         states = [keep.tile([P, T], F32, name="state%d" % b) for b in range(BLOCKS)]
 
         def load_state(b):
             nc.sync.dma_start(states[b][:], rT[b * P : (b + 1) * P, :])
-
-        load_state(0)
 
         picked_scales = keep.tile([P, len(SIDES) * J], U8, name="picked_scales", align_bytes=64)
         for side in SIDES:
@@ -174,37 +176,25 @@ def tile_list_rgg_ownL_kernel(
         )
         edge_scales = (picked_scales[:], moved_scales)
 
-        load_floats(1, (0, 1))
-        load_codes(range(1, 2))
+        load_floats(WO, range(0, 1))
+        weight_rows = keep.tile([P, P], F32, name="weight_rows")
+        nc.sync.dma_start(weight_rows[:], wgo[0 : P * P // J, :].rearrange("r (e p) -> (r e) p", p=P))
+        load_state(0)
         load_state(1)
-        load_floats(2, (0, 1))
-        load_codes(range(2, BLOCKS))
+        load_codes(range(1, BLOCKS))
+        load_floats(WO, range(1, BLOCKS))
         load_state(2)
-        load_floats(3, (0, 1))
         load_state(3)
+        spread_weight = keep.tile([P, HALF], F32, name="spread_weight")
+        nc.sync.dma_start(spread_weight[:], wgo[:, HALF:])
 
-        pick_words(0, "both0")
-        cast(0, 0)
-        cast(0, 1)
-        quantize(0)
-        pick_words(1, "raw101")
+        part_words(pick_words(0, "both0"), 0, "parted0")
+        cast(WB, (0, 1))
+        quantize(WB, (0, 1))
+        second_words = pick_words(1, "stage00")
 
         def bank(kind, u):
             return psum.tile([P, HALF], F32, name="bank", tag="%s%d" % (kind, u % BANKS[kind]))
-
-        turned_weights = bank("back", 1)
-        nc.tensor.transpose(turned_weights[:, 0:P], weight_rows[:], ident[:])
-        edge_weight = keep.tile([P, J // P], F32, name="edge_weight")
-        nc.scalar.copy(edge_weight[:], turned_weights[:, 0 : J // P])
-
-        spread_weight = {}
-        for h in range(1, HALVES):
-            spread = bank("total", h)
-            for e in range(GROUPS):
-                g = h * GROUPS + e
-                nc.tensor.transpose(spread[:, e * P : (e + 1) * P], edge_weight[:, g : g + 1].to_broadcast([P, P]), ident[:])
-            spread_weight[h] = keep.tile([P, HALF], F32, name="spread_weight%d" % h)
-            nc.scalar.copy(spread_weight[h][:], spread[:])
 
         def weight(w, a, b):
             cols = slice(b * P, (b + 1) * P)
@@ -212,9 +202,8 @@ def tile_list_rgg_ownL_kernel(
                 return given_codes[w, b][:, a, :].bitcast(FP4X4), given_scales[:, 0, a, cols]
             if w == "wc":
                 return given_codes[w, b][:, a, :].bitcast(FP8X4), given_scales[:, 1, a, cols]
-            codes, scales = made[b]
-            f = ("wb", "wo").index(w)
-            return codes[:, f, a, :].bitcast(FP8X4), scales[:, f, a, :]
+            codes, scales = made[("wb", "wo").index(w), b]
+            return codes[:, a, :].bitcast(FP8X4), scales[:, a, :]
 
         def product(acc, terms, u):
             b, h = divmod(u, HALVES)
@@ -314,7 +303,7 @@ def tile_list_rgg_ownL_kernel(
 
         def weigh_on_gpsimd(u, total):
             result = result_tile(u)
-            nc.gpsimd.tensor_tensor(result[:], total[:], spread_weight[1][:], MULT)
+            nc.gpsimd.tensor_tensor(result[:], total[:], spread_weight[:], MULT)
             return result
 
         def put(u, result, first=0, count=HALF):
@@ -330,17 +319,23 @@ def tile_list_rgg_ownL_kernel(
         def fresh(pool, name):
             return pool.tile([P, HALF], F32, name=name)[:]
 
+        make_message(0)
+        make_gate(0, (("wb", SRC), ("wa", DST)))
+        cast(WO, (0,))
+        quantize(WO, (0,))
+        make_own(0)
+        part_words(second_words, 1, "raw101")
         pick_state(0, fresh(deep, "residual"))
         pick_state(1, fresh(deep, "residual"))
-        make_message(0)
-        make_gate(0, (("wa", DST), ("wb", SRC)))
-        make_own(0)
-        cast(1, 0)
-        cast(1, 1)
-        quantize(1)
+        cast(WB, (2, 3))
+        quantize(WB, (2, 3))
+        turned_weights = bank("back", 1)
+        nc.tensor.transpose(turned_weights[:, 0:P], weight_rows[:], ident[:])
+        edge_weight = keep.tile([P, J // P], F32, name="edge_weight")
+        nc.scalar.copy(edge_weight[:], turned_weights[:, 0 : J // P])
         pick_state(2, fresh(deep, "residual"))
         pick_state(3, fresh(deep, "residual"))
-        gated0 = keep.tile([P, HALF], F32, name="gated0", tag="raw101", align_bytes=64)[:]
+        gated0 = keep.tile([P, HALF], F32, name="gated0", tag="stage00", align_bytes=64)[:]
         for first in range(0, HALF, HALF // 2):
             let_through(0, gated0, slice(first, first + HALF // 2))
         last = UNITS - 1
@@ -350,7 +345,7 @@ def tile_list_rgg_ownL_kernel(
             make_gate(step, (("wb", SRC), ("wa", DST)))
             make_message(step)
             if step == 1:
-                let_through(step, keep.tile([P, HALF], F32, name="gated1", tag="stage1", align_bytes=64)[:])
+                let_through(step, keep.tile([P, HALF], F32, name="gated1", tag="stage02", align_bytes=64)[:])
             else:
                 let_through(step, fresh(ring, "gated"))
             if step == 1:
@@ -369,11 +364,10 @@ def tile_list_rgg_ownL_kernel(
                 put(step - 1, turn_back(step - 1))
             if step in ON_GPSIMD and step < last:
                 put(step, weigh_on_gpsimd(step, add_on_gpsimd(step)))
-            if step <= 4:
-                b, w = divmod(step - 1, 2)
-                cast(b + 2, w)
-                if w == 1:
-                    quantize(b + 2)
+            if step == 1:
+                for blocks in ((1,), (2, 3)):
+                    cast(WO, blocks)
+                    quantize(WO, blocks)
         page = pages[(BLOCKS - 1) % PAGES]
-        nc.vector.tensor_tensor(page[:].indirect(offsets(DST, HALF, HALF)), add_on_gpsimd(last)[:], spread_weight[1][:], MULT)
+        nc.vector.tensor_tensor(page[:].indirect(offsets(DST, HALF, HALF)), add_on_gpsimd(last)[:], spread_weight[:], MULT)
         nc.sync.dma_start(out[(BLOCKS - 1) * P : BLOCKS * P, :], page[:])

@@ -138,9 +138,9 @@ def tile_list_rgg_ownL_kernel(
                     raw[w, blocks[0], a][:, :, 0:width].rearrange("p i (c m) -> p c i m", m=LINE),
                 )
 
-        def quantize(w, blocks):
+        def quantize(w, blocks, tag=""):
             shape = [P, PASSES, len(blocks) * P]
-            codes = keep.tile(shape, U32, name="codes%d%d" % (w, blocks[0]), align_bytes=64)
+            codes = keep.tile(shape, U32, name="codes", tag=tag or "codes%d%d" % (w, blocks[0]), align_bytes=64)
             scales = keep.tile(shape, U8, name="scales%d%d" % (w, blocks[0]), align_bytes=64)
             nc.vector.quantize_mx(
                 out=codes[:].rearrange("p a n -> p (a n)").bitcast(FP8X4),
@@ -181,8 +181,9 @@ def tile_list_rgg_ownL_kernel(
         nc.sync.dma_start(weight_rows[:], wgo[0 : P * P // J, :].rearrange("r (e p) -> (r e) p", p=P))
         load_state(0)
         load_state(1)
+        load_floats(WO, range(1, 2))
         load_codes(range(1, BLOCKS))
-        load_floats(WO, range(1, BLOCKS))
+        load_floats(WO, range(2, BLOCKS))
         load_state(2)
         load_state(3)
         spread_weight = keep.tile([P, HALF], F32, name="spread_weight")
@@ -241,7 +242,11 @@ def tile_list_rgg_ownL_kernel(
 
         whole_result = keep.tile([P, J], F32, name="whole_result")
 
-        def result_tile(u):
+        def result_tile(u, first=0):
+            if u == 0 and first > 0:
+                return keep.tile([P, HALF], F32, name="result0", tag="raw111", align_bytes=64)
+            if u == 1:
+                return keep.tile([P, HALF], F32, name="result1", tag="raw121", align_bytes=64)
             if u in (4, 5):
                 return whole_result[:, (u - 4) * HALF : (u - 3) * HALF]
             return deep.tile([P, HALF], F32, name="result")
@@ -289,7 +294,7 @@ def tile_list_rgg_ownL_kernel(
             for e in groups:
                 cols = slice(e * P, (e + 1) * P)
                 nc.tensor.transpose(back[:, cols], weighted[u, groups[0]][:, cols], ident[:])
-            result = result_tile(u)
+            result = result_tile(u, groups[0])
             cols = slice(groups[0] * P, (groups[-1] + 1) * P)
             nc.scalar.copy(result[:, cols], back[:, cols])
             return result
@@ -328,7 +333,7 @@ def tile_list_rgg_ownL_kernel(
         pick_state(0, fresh(deep, "residual"))
         pick_state(1, fresh(deep, "residual"))
         cast(WB, (2, 3))
-        quantize(WB, (2, 3))
+        quantize(WB, (2, 3), "stage10")
         turned_weights = bank("back", 1)
         nc.tensor.transpose(turned_weights[:, 0:P], weight_rows[:], ident[:])
         edge_weight = keep.tile([P, J // P], F32, name="edge_weight")
@@ -338,6 +343,9 @@ def tile_list_rgg_ownL_kernel(
         gated0 = keep.tile([P, HALF], F32, name="gated0", tag="stage00", align_bytes=64)[:]
         for first in range(0, HALF, HALF // 2):
             let_through(0, gated0, slice(first, first + HALF // 2))
+        for blocks in ((1,), (2, 3)):
+            cast(WO, blocks)
+            quantize(WO, blocks)
         last = UNITS - 1
         for step in range(1, UNITS):
             if step in ON_GPSIMD:
@@ -364,10 +372,6 @@ def tile_list_rgg_ownL_kernel(
                 put(step - 1, turn_back(step - 1))
             if step in ON_GPSIMD and step < last:
                 put(step, weigh_on_gpsimd(step, add_on_gpsimd(step)))
-            if step == 1:
-                for blocks in ((1,), (2, 3)):
-                    cast(WO, blocks)
-                    quantize(WO, blocks)
         page = pages[(BLOCKS - 1) % PAGES]
         nc.vector.tensor_tensor(page[:].indirect(offsets(DST, HALF, HALF)), add_on_gpsimd(last)[:], spread_weight[:], MULT)
         nc.sync.dma_start(out[(BLOCKS - 1) * P : BLOCKS * P, :], page[:])

@@ -39,6 +39,8 @@ UNITS = BLOCKS * HALVES
 GROUPS = HALF // P
 ON_GPSIMD = (5, 7)
 WB, WO = 0, 1
+ORDER = ((0, 0), (0, 1), (1, 0), (1, 1), (2, 0), (3, 0), (2, 1), (3, 1))
+PAGE_OF = (0, 1, 0, 2)
 BANKS = {"gate": 2, "message": 1, "own": 1, "total": 2, "back": 2}
 
 
@@ -186,8 +188,8 @@ def tile_list_rgg_ownL_kernel(
         load_floats(WO, range(2, BLOCKS))
         load_state(2)
         load_state(3)
-        spread_weight = keep.tile([P, HALF], F32, name="spread_weight")
-        nc.sync.dma_start(spread_weight[:], wgo[:, HALF:])
+        spread_weight = keep.tile([P, J], F32, name="spread_weight")
+        nc.sync.dma_start(spread_weight[:], wgo)
 
         part_words(pick_words(0, "both0"), 0, "parted0")
         cast(WB, (0, 1))
@@ -207,7 +209,7 @@ def tile_list_rgg_ownL_kernel(
             return codes[:, a, :].bitcast(FP8X4), scales[:, a, :]
 
         def product(acc, terms, u):
-            b, h = divmod(u, HALVES)
+            b, h = ORDER[u]
             steps = [(w, side, a) for w, side in terms for a in reversed(range(PASSES))]
             for s, (w, side, a) in enumerate(steps):
                 codes, scales = weight(w, a, b)
@@ -230,7 +232,7 @@ def tile_list_rgg_ownL_kernel(
         weighted = {}
 
         def pick_state(u, target):
-            b, h = divmod(u, HALVES)
+            b, h = ORDER[u]
             residual[u] = target
             nc.vector.tensor_copy(target, states[b][:].indirect(offsets(DST, h * HALF, HALF)))
 
@@ -238,23 +240,22 @@ def tile_list_rgg_ownL_kernel(
             whole = keep.tile([P, J], F32, name="residual_block%d" % b)
             nc.vector.tensor_copy(whole[:], states[b][:].indirect(dst_list[:]))
             for h in range(HALVES):
-                residual[b * HALVES + h] = whole[:, h * HALF : (h + 1) * HALF]
-
-        whole_result = keep.tile([P, J], F32, name="whole_result")
+                residual[ORDER.index((b, h))] = whole[:, h * HALF : (h + 1) * HALF]
 
         def result_tile(u, first=0):
             if u == 0 and first > 0:
                 return keep.tile([P, HALF], F32, name="result0", tag="raw111", align_bytes=64)
             if u == 1:
                 return keep.tile([P, HALF], F32, name="result1", tag="raw121", align_bytes=64)
-            if u in (4, 5):
-                return whole_result[:, (u - 4) * HALF : (u - 3) * HALF]
             return deep.tile([P, HALF], F32, name="result")
 
         def make_gate(u, terms):
             gate_sum = bank("gate", u)
             product(gate_sum, terms, u)
-            gate[u] = ring.tile([P, HALF], F32, name="gate")
+            if u == 3:
+                gate[u] = keep.tile([P, HALF], F32, name="gate3", tag="page2")
+            else:
+                gate[u] = ring.tile([P, HALF], F32, name="gate")
             nc.scalar.activation(gate[u][:], gate_sum[:], SIGMOID)
 
         def make_message(u):
@@ -286,7 +287,7 @@ def tile_list_rgg_ownL_kernel(
             weighted[u, groups[0]] = ring.tile([P, HALF], F32, name="weighted")
             for e in groups:
                 cols = slice(e * P, (e + 1) * P)
-                g = (u % HALVES) * GROUPS + e
+                g = ORDER[u][1] * GROUPS + e
                 nc.scalar.activation(weighted[u, groups[0]][:, cols], total[:, cols], COPY, scale=edge_weight[:, g : g + 1])
 
         def turn_back(u, groups=range(GROUPS)):
@@ -308,16 +309,13 @@ def tile_list_rgg_ownL_kernel(
 
         def weigh_on_gpsimd(u, total):
             result = result_tile(u)
-            nc.gpsimd.tensor_tensor(result[:], total[:], spread_weight[:], MULT)
+            nc.gpsimd.tensor_tensor(result[:], total[:], spread_weight[:, 0:HALF], MULT)
             return result
 
         def put(u, result, first=0, count=HALF):
-            b, h = divmod(u, HALVES)
-            page = pages[b % PAGES]
-            if u == 5:
-                nc.vector.tensor_copy(page[:].indirect(dst_list[:]), whole_result[:])
-            elif u != 4:
-                nc.vector.tensor_copy(page[:].indirect(offsets(DST, h * HALF + first, count)), result[:, first : first + count])
+            b, h = ORDER[u]
+            page = pages[PAGE_OF[b]]
+            nc.vector.tensor_copy(page[:].indirect(offsets(DST, h * HALF + first, count)), result[:, first : first + count])
             if h == HALVES - 1:
                 nc.sync.dma_start(out[b * P : (b + 1) * P, :], page[:])
 
@@ -363,6 +361,9 @@ def tile_list_rgg_ownL_kernel(
                 add_up(step - 1)
             if step in (1, 3):
                 pick_block_state(step // 2 + 2)
+            if step == 3:
+                pages.append(keep.tile([P, T], F32, name="page2", tag="page2"))
+                nc.gpsimd.memset(pages[2][:].bitcast(I32), 0)
             if step not in ON_GPSIMD:
                 make_own(step)
             if step == 1:
@@ -372,6 +373,6 @@ def tile_list_rgg_ownL_kernel(
                 put(step - 1, turn_back(step - 1))
             if step in ON_GPSIMD and step < last:
                 put(step, weigh_on_gpsimd(step, add_on_gpsimd(step)))
-        page = pages[(BLOCKS - 1) % PAGES]
-        nc.vector.tensor_tensor(page[:].indirect(offsets(DST, HALF, HALF)), add_on_gpsimd(last)[:], spread_weight[:], MULT)
+        page = pages[PAGE_OF[BLOCKS - 1]]
+        nc.vector.tensor_tensor(page[:].indirect(offsets(DST, HALF, HALF)), add_on_gpsimd(last)[:], spread_weight[:, HALF:], MULT)
         nc.sync.dma_start(out[(BLOCKS - 1) * P : BLOCKS * P, :], page[:])

@@ -152,12 +152,12 @@ def tile_list_rgg_ownL_kernel(
             for i, b in enumerate(blocks):
                 made[w, b] = (codes[:, :, i * P : (i + 1) * P], scales[:, :, i * P : (i + 1) * P])
 
-        nc.sync.dma_start(dst_list[:], offs2)
         for r in range(ROWS):
             nc.sync.dma_start(
                 table_scales[r : P : SHIFT, :].bitcast(I32),
                 tab_scales.rearrange("a (q r) t -> r q a t", r=ROWS)[r].bitcast(I32),
             )
+        nc.sync.dma_start(dst_list[:], offs2)
         nc.sync.dma_start(src_list[:], offs)
         table_words = keep.tile([P, T], I32, name="table_words", align_bytes=64)
         nc.sync.dma_start(table_words[:], tab_words[0].rearrange("p t b -> p (t b)").bitcast(I32))
@@ -336,8 +336,7 @@ def tile_list_rgg_ownL_kernel(
         nc.tensor.transpose(turned_weights[:, 0:P], weight_rows[:], ident[:])
         edge_weight = keep.tile([P, J // P], F32, name="edge_weight")
         nc.scalar.copy(edge_weight[:], turned_weights[:, 0 : J // P])
-        pick_state(2, fresh(deep, "residual"))
-        pick_state(3, fresh(deep, "residual"))
+        pick_block_state(1)
         gated0 = keep.tile([P, HALF], F32, name="gated0", tag="stage00", align_bytes=64)[:]
         for first in range(0, HALF, HALF // 2):
             let_through(0, gated0, slice(first, first + HALF // 2))
@@ -350,8 +349,9 @@ def tile_list_rgg_ownL_kernel(
                 make_own(step)
             make_gate(step, (("wb", SRC), ("wa", DST)))
             make_message(step)
-            if step == 1:
-                let_through(step, keep.tile([P, HALF], F32, name="gated1", tag="stage02", align_bytes=64)[:])
+            if step <= 3:
+                tag = ("stage02", "stage11", "stage12")[step - 1]
+                let_through(step, keep.tile([P, HALF], F32, name="gated", tag=tag, align_bytes=64)[:])
             else:
                 let_through(step, fresh(ring, "gated"))
             if step == 1:

@@ -184,12 +184,13 @@ def tile_list_rgg_ownL_kernel(
         load_state(0)
         load_state(1)
         load_floats(WO, range(1, 2))
+        load_state(2)
+        spread_weight = [keep.tile([P, HALF], F32, name="spread_weight%d" % h) for h in range(HALVES)]
+        nc.sync.dma_start(spread_weight[1][:], wgo[:, HALF:J])
         load_codes(range(1, BLOCKS))
         load_floats(WO, range(2, BLOCKS))
-        load_state(2)
         load_state(3)
-        spread_weight = keep.tile([P, J], F32, name="spread_weight")
-        nc.sync.dma_start(spread_weight[:], wgo)
+        nc.sync.dma_start(spread_weight[0][:], wgo[:, 0:HALF])
 
         part_words(pick_words(0, "both0"), 0, "parted0")
         cast(WB, (0, 1))
@@ -245,8 +246,8 @@ def tile_list_rgg_ownL_kernel(
         def result_tile(u, first=0):
             if u == 0 and first > 0:
                 return keep.tile([P, HALF], F32, name="result0", tag="raw111", align_bytes=64)
-            if u == 1:
-                return keep.tile([P, HALF], F32, name="result1", tag="raw121", align_bytes=64)
+            if u == 2:
+                return keep.tile([P, HALF], F32, name="result2", tag="raw121", align_bytes=64)
             return deep.tile([P, HALF], F32, name="result")
 
         def make_gate(u, terms):
@@ -287,8 +288,8 @@ def tile_list_rgg_ownL_kernel(
             weighted[u, groups[0]] = ring.tile([P, HALF], F32, name="weighted")
             for e in groups:
                 cols = slice(e * P, (e + 1) * P)
-                g = ORDER[u][1] * GROUPS + e
-                nc.scalar.activation(weighted[u, groups[0]][:, cols], total[:, cols], COPY, scale=edge_weight[:, g : g + 1])
+                scale = edge_weight[ORDER[u][1]][:, e : e + 1]
+                nc.scalar.activation(weighted[u, groups[0]][:, cols], total[:, cols], COPY, scale=scale)
 
         def turn_back(u, groups=range(GROUPS)):
             back = bank("back", u + groups[0] // 2)
@@ -309,7 +310,7 @@ def tile_list_rgg_ownL_kernel(
 
         def weigh_on_gpsimd(u, total):
             result = result_tile(u)
-            nc.gpsimd.tensor_tensor(result[:], total[:], spread_weight[:, 0:HALF], MULT)
+            nc.gpsimd.tensor_tensor(result[:], total[:], spread_weight[0][:], MULT)
             return result
 
         def put(u, result, first=0, count=HALF):
@@ -334,8 +335,8 @@ def tile_list_rgg_ownL_kernel(
         quantize(WB, (2, 3), "stage10")
         turned_weights = bank("back", 1)
         nc.tensor.transpose(turned_weights[:, 0:P], weight_rows[:], ident[:])
-        edge_weight = keep.tile([P, J // P], F32, name="edge_weight")
-        nc.scalar.copy(edge_weight[:], turned_weights[:, 0 : J // P])
+        edge_weight = [keep.tile([P, GROUPS], F32, name="edge_weight%d" % h) for h in range(HALVES)]
+        nc.scalar.copy(edge_weight[0][:], turned_weights[:, 0:GROUPS])
         pick_block_state(1)
         gated0 = keep.tile([P, HALF], F32, name="gated0", tag="stage00", align_bytes=64)[:]
         for first in range(0, HALF, HALF // 2):
@@ -349,11 +350,17 @@ def tile_list_rgg_ownL_kernel(
                 make_own(step)
             make_gate(step, (("wb", SRC), ("wa", DST)))
             make_message(step)
-            if step <= 3:
-                tag = ("stage02", "stage11", "stage12")[step - 1]
+            if step <= 2:
+                tag = ("stage02", "stage11")[step - 1]
                 let_through(step, keep.tile([P, HALF], F32, name="gated", tag=tag, align_bytes=64)[:])
             else:
                 let_through(step, fresh(ring, "gated"))
+            if step == 2:
+                turned_weights = bank("total", 0)
+                for e in range(GROUPS):
+                    cols = slice(e * P, (e + 1) * P)
+                    nc.tensor.transpose(turned_weights[:, cols], spread_weight[1][:, cols], ident[:])
+                nc.scalar.copy(edge_weight[1][:], turned_weights[:, 0:HALF:P])
             if step == 1:
                 add_up(0, range(0, 2))
                 add_up(0, range(2, 4))
@@ -374,5 +381,5 @@ def tile_list_rgg_ownL_kernel(
             if step in ON_GPSIMD and step < last:
                 put(step, weigh_on_gpsimd(step, add_on_gpsimd(step)))
         page = pages[PAGE_OF[BLOCKS - 1]]
-        nc.vector.tensor_tensor(page[:].indirect(offsets(DST, HALF, HALF)), add_on_gpsimd(last)[:], spread_weight[:, HALF:], MULT)
+        nc.vector.tensor_tensor(page[:].indirect(offsets(DST, HALF, HALF)), add_on_gpsimd(last)[:], spread_weight[1][:], MULT)
         nc.sync.dma_start(out[(BLOCKS - 1) * P : BLOCKS * P, :], page[:])

@@ -30,14 +30,14 @@ LINE = 4
 HALF = 512
 HALVES = J // HALF
 BLOCKS = N // P
-PAGES = 2
+PAGES = 3
 SHIFT = QUAD // PASSES
 MOVED_ROWS = 112
 DST, SRC = 0, 1
 SIDES = (DST, SRC)
 UNITS = BLOCKS * HALVES
 GROUPS = HALF // P
-ON_GPSIMD = (5, 7)
+ON_GPSIMD = (1, 5, 7)
 WB, WO = 0, 1
 ORDER = ((0, 0), (0, 1), (1, 0), (1, 1), (2, 0), (3, 0), (2, 1), (3, 1))
 PAGE_OF = (0, 1, 0, 2)
@@ -63,15 +63,14 @@ def tile_list_rgg_ownL_kernel(
 
         table_scales = keep.tile([P, T], U8, name="table_scales", align_bytes=64)
         nc.gpsimd.memset(table_scales[:].bitcast(I32), 0)
+        warm = keep.tile([P, 2], F32, name="warm")
+        nc.gpsimd.memset(warm[:, 0:1], 0.0)
         planes = keep.tile([P, 2 * PASSES * N + len(SIDES) * J], U8, name="planes", align_bytes=64)
         nc.gpsimd.memset(planes[:].bitcast(I32), 0)
         given_scales = planes[:, 0 : 2 * PASSES * N].rearrange("p (w a n) -> p w a n", w=2, a=PASSES)
         moved_scales = planes[:, 2 * PASSES * N :]
         ident = keep.tile([P, P], F32, name="ident")
         make_identity(nc, ident[:])
-        warm = keep.tile([P, 2], F32, name="warm")
-        nc.vector.memset(warm[:, 0:1], 0.0)
-        nc.scalar.activation(warm[:, 1:2], warm[:, 0:1], SIGMOID)
         pages = [keep.tile([P, T], F32, name="page%d" % i) for i in range(PAGES)]
         for page in pages:
             nc.gpsimd.memset(page[:].bitcast(I32), 0)
@@ -153,10 +152,11 @@ def tile_list_rgg_ownL_kernel(
                 made[w, b] = (codes[:, :, i * P : (i + 1) * P], scales[:, :, i * P : (i + 1) * P])
 
         for r in range(ROWS):
-            nc.sync.dma_start(
+            (nc.sync, nc.scalar)[r % 2].dma_start(
                 table_scales[r : P : SHIFT, :].bitcast(I32),
                 tab_scales.rearrange("a (q r) t -> r q a t", r=ROWS)[r].bitcast(I32),
             )
+        nc.scalar.activation(warm[:, 1:2], warm[:, 0:1], SIGMOID)
         nc.sync.dma_start(dst_list[:], offs2)
         nc.sync.dma_start(src_list[:], offs)
         table_words = keep.tile([P, T], I32, name="table_words", align_bytes=64)
@@ -184,10 +184,10 @@ def tile_list_rgg_ownL_kernel(
         load_state(0)
         load_state(1)
         load_floats(WO, range(1, 2))
+        load_codes(range(1, BLOCKS))
         load_state(2)
         spread_weight = [keep.tile([P, HALF], F32, name="spread_weight%d" % h) for h in range(HALVES)]
         nc.sync.dma_start(spread_weight[1][:], wgo[:, HALF:J])
-        load_codes(range(1, BLOCKS))
         load_floats(WO, range(2, BLOCKS))
         load_state(3)
         nc.sync.dma_start(spread_weight[0][:], wgo[:, 0:HALF])
@@ -246,17 +246,14 @@ def tile_list_rgg_ownL_kernel(
         def result_tile(u, first=0):
             if u == 0 and first > 0:
                 return keep.tile([P, HALF], F32, name="result0", tag="raw111", align_bytes=64)
-            if u == 2:
-                return keep.tile([P, HALF], F32, name="result2", tag="raw121", align_bytes=64)
+            if u == 1:
+                return keep.tile([P, HALF], F32, name="result1", tag="stage11", align_bytes=64)
             return deep.tile([P, HALF], F32, name="result")
 
         def make_gate(u, terms):
             gate_sum = bank("gate", u)
             product(gate_sum, terms, u)
-            if u == 3:
-                gate[u] = keep.tile([P, HALF], F32, name="gate3", tag="page2")
-            else:
-                gate[u] = ring.tile([P, HALF], F32, name="gate")
+            gate[u] = ring.tile([P, HALF], F32, name="gate")
             nc.scalar.activation(gate[u][:], gate_sum[:], SIGMOID)
 
         def make_message(u):
@@ -285,10 +282,14 @@ def tile_list_rgg_ownL_kernel(
                         total[:, cols], lhsT=term[:, cols], rhs=ident[:], is_transpose=True,
                         start=(s == 0), stop=(s == len(terms) - 1),
                     )
-            weighted[u, groups[0]] = ring.tile([P, HALF], F32, name="weighted")
+            if u == 2:
+                weighted[u, 0] = keep.tile([P, HALF], F32, name="weighted2", tag="raw121", align_bytes=64)
+            else:
+                weighted[u, groups[0]] = ring.tile([P, HALF], F32, name="weighted")
             for e in groups:
                 cols = slice(e * P, (e + 1) * P)
-                scale = edge_weight[ORDER[u][1]][:, e : e + 1]
+                g = ORDER[u][1] * GROUPS + e
+                scale = edge_weight[:, g : g + 1]
                 nc.scalar.activation(weighted[u, groups[0]][:, cols], total[:, cols], COPY, scale=scale)
 
         def turn_back(u, groups=range(GROUPS)):
@@ -310,7 +311,7 @@ def tile_list_rgg_ownL_kernel(
 
         def weigh_on_gpsimd(u, total):
             result = result_tile(u)
-            nc.gpsimd.tensor_tensor(result[:], total[:], spread_weight[0][:], MULT)
+            nc.gpsimd.tensor_tensor(result[:], total[:], spread_weight[ORDER[u][1]][:], MULT)
             return result
 
         def put(u, result, first=0, count=HALF):
@@ -335,32 +336,23 @@ def tile_list_rgg_ownL_kernel(
         quantize(WB, (2, 3), "stage10")
         turned_weights = bank("back", 1)
         nc.tensor.transpose(turned_weights[:, 0:P], weight_rows[:], ident[:])
-        edge_weight = [keep.tile([P, GROUPS], F32, name="edge_weight%d" % h) for h in range(HALVES)]
-        nc.scalar.copy(edge_weight[0][:], turned_weights[:, 0:GROUPS])
+        edge_weight = keep.tile([P, J // P], F32, name="edge_weight")
+        nc.scalar.copy(edge_weight[:], turned_weights[:, 0 : J // P])
         pick_block_state(1)
         gated0 = keep.tile([P, HALF], F32, name="gated0", tag="stage00", align_bytes=64)[:]
         for first in range(0, HALF, HALF // 2):
             let_through(0, gated0, slice(first, first + HALF // 2))
-        for blocks in ((1,), (2, 3)):
-            cast(WO, blocks)
-            quantize(WO, blocks)
         last = UNITS - 1
         for step in range(1, UNITS):
-            if step in ON_GPSIMD:
+            if step in ON_GPSIMD and step > 1:
                 make_own(step)
             make_gate(step, (("wb", SRC), ("wa", DST)))
             make_message(step)
-            if step <= 2:
-                tag = ("stage02", "stage11")[step - 1]
+            if step <= 1:
+                tag = "stage02"
                 let_through(step, keep.tile([P, HALF], F32, name="gated", tag=tag, align_bytes=64)[:])
             else:
                 let_through(step, fresh(ring, "gated"))
-            if step == 2:
-                turned_weights = bank("total", 0)
-                for e in range(GROUPS):
-                    cols = slice(e * P, (e + 1) * P)
-                    nc.tensor.transpose(turned_weights[:, cols], spread_weight[1][:, cols], ident[:])
-                nc.scalar.copy(edge_weight[1][:], turned_weights[:, 0:HALF:P])
             if step == 1:
                 add_up(0, range(0, 2))
                 add_up(0, range(2, 4))
@@ -368,13 +360,13 @@ def tile_list_rgg_ownL_kernel(
                 add_up(step - 1)
             if step in (1, 3):
                 pick_block_state(step // 2 + 2)
-            if step == 3:
-                pages.append(keep.tile([P, T], F32, name="page2", tag="page2"))
-                nc.gpsimd.memset(pages[2][:].bitcast(I32), 0)
-            if step not in ON_GPSIMD:
+            if step not in ON_GPSIMD or step == 1:
                 make_own(step)
             if step == 1:
                 put(0, turn_back(0, range(0, 2)), 0, HALF // 2)
+                for blocks in ((1,), (2, 3)):
+                    cast(WO, blocks)
+                    quantize(WO, blocks)
                 put(0, turn_back(0, range(2, 4)), HALF // 2, HALF // 2)
             elif step - 1 not in ON_GPSIMD:
                 put(step - 1, turn_back(step - 1))

@@ -37,7 +37,7 @@ DST, SRC = 0, 1
 SIDES = (DST, SRC)
 UNITS = BLOCKS * HALVES
 GROUPS = HALF // P
-ON_GPSIMD = (1, 5, 7)
+ON_GPSIMD = (1, 3, 5, 7)
 WB, WO = 0, 1
 ORDER = ((0, 0), (0, 1), (1, 0), (1, 1), (2, 0), (3, 0), (2, 1), (3, 1))
 PAGE_OF = (0, 1, 0, 2)
@@ -152,7 +152,7 @@ def tile_list_rgg_ownL_kernel(
                 made[w, b] = (codes[:, :, i * P : (i + 1) * P], scales[:, :, i * P : (i + 1) * P])
 
         for r in range(ROWS):
-            (nc.sync, nc.scalar)[r % 2].dma_start(
+            nc.sync.dma_start(
                 table_scales[r : P : SHIFT, :].bitcast(I32),
                 tab_scales.rearrange("a (q r) t -> r q a t", r=ROWS)[r].bitcast(I32),
             )

@@ -37,7 +37,7 @@ DST, SRC = 0, 1
 SIDES = (DST, SRC)
 UNITS = BLOCKS * HALVES
 GROUPS = HALF // P
-ON_GPSIMD = (1, 3, 5, 7)
+ON_GPSIMD = (1, 5, 7)
 WB, WO = 0, 1
 ORDER = ((0, 0), (0, 1), (1, 0), (1, 1), (2, 0), (3, 0), (2, 1), (3, 1))
 PAGE_OF = (0, 1, 0, 2)
@@ -246,8 +246,6 @@ def tile_list_rgg_ownL_kernel(
         def result_tile(u, first=0):
             if u == 0 and first > 0:
                 return keep.tile([P, HALF], F32, name="result0", tag="raw111", align_bytes=64)
-            if u == 1:
-                return keep.tile([P, HALF], F32, name="result1", tag="stage11", align_bytes=64)
             return deep.tile([P, HALF], F32, name="result")
 
         def make_gate(u, terms):
@@ -269,7 +267,10 @@ def tile_list_rgg_ownL_kernel(
         def make_own(u):
             own_sum = bank("own", u)
             product(own_sum, (("wo", DST),), u)
-            own[u] = ring.tile([P, HALF], F32, name="own")
+            if u == 1:
+                own[u] = keep.tile([P, HALF], F32, name="own1", tag="weighted0")
+            else:
+                own[u] = ring.tile([P, HALF], F32, name="own")
             nc.scalar.copy(own[u][:], own_sum[:])
 
         def add_up(u, groups=range(GROUPS)):
@@ -282,7 +283,9 @@ def tile_list_rgg_ownL_kernel(
                         total[:, cols], lhsT=term[:, cols], rhs=ident[:], is_transpose=True,
                         start=(s == 0), stop=(s == len(terms) - 1),
                     )
-            if u == 2:
+            if u == 0 and groups[0] == 0:
+                weighted[u, 0] = keep.tile([P, HALF], F32, name="weighted0", tag="weighted0")
+            elif u == 2:
                 weighted[u, 0] = keep.tile([P, HALF], F32, name="weighted2", tag="raw121", align_bytes=64)
             else:
                 weighted[u, groups[0]] = ring.tile([P, HALF], F32, name="weighted")
@@ -304,9 +307,13 @@ def tile_list_rgg_ownL_kernel(
 
         def add_on_gpsimd(u):
             partial = ring.tile([P, HALF], F32, name="partial")
-            nc.gpsimd.tensor_tensor(partial[:], own[u][:], residual[u], ADD)
-            total = ring.tile([P, HALF], F32, name="partial")
-            nc.gpsimd.tensor_tensor(total[:], partial[:], gated[u], ADD)
+            first, second = (gated[u], own[u][:]) if u == 1 else (own[u][:], gated[u])
+            nc.gpsimd.tensor_tensor(partial[:], first, residual[u], ADD)
+            if u == 1:
+                total = keep.tile([P, HALF], F32, name="total1", tag="stage11", align_bytes=64)
+            else:
+                total = ring.tile([P, HALF], F32, name="partial")
+            nc.gpsimd.tensor_tensor(total[:], partial[:], second, ADD)
             return total
 
         def weigh_on_gpsimd(u, total):
@@ -333,7 +340,6 @@ def tile_list_rgg_ownL_kernel(
         pick_state(0, fresh(deep, "residual"))
         pick_state(1, fresh(deep, "residual"))
         cast(WB, (2, 3))
-        quantize(WB, (2, 3), "stage10")
         turned_weights = bank("back", 1)
         nc.tensor.transpose(turned_weights[:, 0:P], weight_rows[:], ident[:])
         edge_weight = keep.tile([P, J // P], F32, name="edge_weight")
@@ -348,8 +354,8 @@ def tile_list_rgg_ownL_kernel(
                 make_own(step)
             make_gate(step, (("wb", SRC), ("wa", DST)))
             make_message(step)
-            if step <= 1:
-                tag = "stage02"
+            if step == 4:
+                tag = "stage12"
                 let_through(step, keep.tile([P, HALF], F32, name="gated", tag=tag, align_bytes=64)[:])
             else:
                 let_through(step, fresh(ring, "gated"))
@@ -360,13 +366,16 @@ def tile_list_rgg_ownL_kernel(
                 add_up(step - 1)
             if step in (1, 3):
                 pick_block_state(step // 2 + 2)
-            if step not in ON_GPSIMD or step == 1:
+            if step not in ON_GPSIMD:
                 make_own(step)
             if step == 1:
                 put(0, turn_back(0, range(0, 2)), 0, HALF // 2)
-                for blocks in ((1,), (2, 3)):
-                    cast(WO, blocks)
-                    quantize(WO, blocks)
+                make_own(step)
+                cast(WO, (1,))
+                quantize(WB, (2, 3), "raw110")
+                quantize(WO, (1,))
+                cast(WO, (2, 3))
+                quantize(WO, (2, 3))
                 put(0, turn_back(0, range(2, 4)), HALF // 2, HALF // 2)
             elif step - 1 not in ON_GPSIMD:
                 put(step - 1, turn_back(step - 1))

@@ -78,8 +78,8 @@ def tile_list_rgg_ownL_kernel(
         float_weights = (wb, wo)
         raw = {}
 
-        def load_floats(w, blocks):
-            for a in range(PASSES):
+        def load_floats(w, blocks, passes=range(PASSES)):
+            for a in passes:
                 name = "raw%d%d%d" % (w, blocks[0], a)
                 t = keep.tile([P, PACK, len(blocks) * P], F32, name=name, tag=name, align_bytes=64)
                 rows = float_weights[w][a * P * PACK : (a + 1) * P * PACK, blocks[0] * P : (blocks[-1] + 1) * P]
@@ -151,20 +151,21 @@ def tile_list_rgg_ownL_kernel(
             for i, b in enumerate(blocks):
                 made[w, b] = (codes[:, :, i * P : (i + 1) * P], scales[:, :, i * P : (i + 1) * P])
 
+        nc.sync.dma_start(dst_list[:], offs2)
+        weight_rows = keep.tile([P, P], F32, name="weight_rows")
+        nc.sync.dma_start(weight_rows[:], wgo[0 : P * P // J, :].rearrange("r (e p) -> (r e) p", p=P))
+        nc.sync.dma_start(src_list[:], offs)
         for r in range(ROWS):
             nc.sync.dma_start(
                 table_scales[r : P : SHIFT, :].bitcast(I32),
                 tab_scales.rearrange("a (q r) t -> r q a t", r=ROWS)[r].bitcast(I32),
             )
         nc.scalar.activation(warm[:, 1:2], warm[:, 0:1], SIGMOID)
-        nc.sync.dma_start(dst_list[:], offs2)
-        nc.sync.dma_start(src_list[:], offs)
         table_words = keep.tile([P, T], I32, name="table_words", align_bytes=64)
         nc.sync.dma_start(table_words[:], tab_words[0].rearrange("p t b -> p (t b)").bitcast(I32))
         load_scales(1, wc_scales)
         load_floats(WB, range(BLOCKS))
         load_codes(range(0, 1))
-        load_scales(0, wa_scales)
         states = [keep.tile([P, T], F32, name="state%d" % b) for b in range(BLOCKS)]
 
         def load_state(b):
@@ -178,9 +179,9 @@ def tile_list_rgg_ownL_kernel(
         )
         edge_scales = (picked_scales[:], moved_scales)
 
-        load_floats(WO, range(0, 1))
-        weight_rows = keep.tile([P, P], F32, name="weight_rows")
-        nc.sync.dma_start(weight_rows[:], wgo[0 : P * P // J, :].rearrange("r (e p) -> (r e) p", p=P))
+        load_floats(WO, range(0, 1), range(0, 1))
+        load_scales(0, wa_scales)
+        load_floats(WO, range(0, 1), range(1, 2))
         load_state(0)
         load_state(1)
         load_floats(WO, range(1, 2))

@@ -129,27 +129,30 @@ def tile_list_rgg_ownL_kernel(
         grouped = {}
         made = {}
 
-        def cast(w, blocks):
+        def cast(w, blocks, passes=range(PASSES), tag=""):
             name = "stage%d%d" % (w, blocks[0])
             width = len(blocks) * P
-            grouped[w, blocks] = keep.tile([P, PASSES, width, PACK], BF16, name=name, tag=name, align_bytes=64)
-            for a in range(PASSES):
+            t = keep.tile([P, len(passes), width, PACK], BF16, name=name, tag=tag or name, align_bytes=64)
+            grouped[w, blocks, passes] = t
+            for i, a in enumerate(passes):
                 nc.scalar.copy(
-                    grouped[w, blocks][:, a].rearrange("p (c m) i -> p c i m", m=LINE),
+                    t[:, i].rearrange("p (c m) i -> p c i m", m=LINE),
                     raw[w, blocks[0], a][:, :, 0:width].rearrange("p i (c m) -> p c i m", m=LINE),
                 )
 
-        def quantize(w, blocks, tag=""):
-            shape = [P, PASSES, len(blocks) * P]
-            codes = keep.tile(shape, U32, name="codes", tag=tag or "codes%d%d" % (w, blocks[0]), align_bytes=64)
-            scales = keep.tile(shape, U8, name="scales%d%d" % (w, blocks[0]), align_bytes=64)
+        def quantize(w, blocks, passes=range(PASSES), tag=""):
+            shape = [P, len(passes), len(blocks) * P]
+            name = "%d%d%d" % (w, blocks[0], passes[0])
+            codes = keep.tile(shape, U32, name="codes" + name, tag=tag or "codes" + name, align_bytes=64)
+            scales = keep.tile(shape, U8, name="scales" + name, align_bytes=64)
             nc.vector.quantize_mx(
                 out=codes[:].rearrange("p a n -> p (a n)").bitcast(FP8X4),
                 scales=scales[:].rearrange("p a n -> p (a n)"),
-                in_=grouped[w, blocks][:].rearrange("p a n i -> p (a n i)"),
+                in_=grouped[w, blocks, passes][:].rearrange("p a n i -> p (a n i)"),
             )
             for i, b in enumerate(blocks):
-                made[w, b] = (codes[:, :, i * P : (i + 1) * P], scales[:, :, i * P : (i + 1) * P])
+                for n, a in enumerate(passes):
+                    made[w, b, a] = (codes[:, n, i * P : (i + 1) * P], scales[:, n, i * P : (i + 1) * P])
 
         nc.sync.dma_start(dst_list[:], offs2)
         weight_rows = keep.tile([P, P], F32, name="weight_rows")
@@ -196,6 +199,8 @@ def tile_list_rgg_ownL_kernel(
         part_words(pick_words(0, "both0"), 0, "parted0")
         cast(WB, (0, 1))
         quantize(WB, (0, 1))
+        cast(WB, (2, 3), range(0, 1))
+        quantize(WB, (2, 3), range(0, 1))
         second_words = pick_words(1, "stage00")
 
         def bank(kind, u):
@@ -207,8 +212,8 @@ def tile_list_rgg_ownL_kernel(
                 return given_codes[w, b][:, a, :].bitcast(FP4X4), given_scales[:, 0, a, cols]
             if w == "wc":
                 return given_codes[w, b][:, a, :].bitcast(FP8X4), given_scales[:, 1, a, cols]
-            codes, scales = made[("wb", "wo").index(w), b]
-            return codes[:, a, :].bitcast(FP8X4), scales[:, a, :]
+            codes, scales = made[("wb", "wo").index(w), b, a]
+            return codes.bitcast(FP8X4), scales
 
         def product(acc, terms, u):
             b, h = ORDER[u]
@@ -340,7 +345,7 @@ def tile_list_rgg_ownL_kernel(
         part_words(second_words, 1, "raw101")
         pick_state(0, fresh(deep, "residual"))
         pick_state(1, fresh(deep, "residual"))
-        cast(WB, (2, 3))
+        cast(WB, (2, 3), range(1, 2), "stage10")
         turned_weights = bank("back", 1)
         nc.tensor.transpose(turned_weights[:, 0:P], weight_rows[:], ident[:])
         edge_weight = keep.tile([P, J // P], F32, name="edge_weight")
@@ -373,7 +378,7 @@ def tile_list_rgg_ownL_kernel(
                 put(0, turn_back(0, range(0, 2)), 0, HALF // 2)
                 make_own(step)
                 cast(WO, (1,))
-                quantize(WB, (2, 3), "raw110")
+                quantize(WB, (2, 3), range(1, 2), "raw110")
                 quantize(WO, (1,))
                 cast(WO, (2, 3))
                 quantize(WO, (2, 3))

@@ -197,10 +197,10 @@ def tile_list_rgg_ownL_kernel(
         nc.sync.dma_start(spread_weight[0][:], wgo[:, 0:HALF])
 
         part_words(pick_words(0, "both0"), 0, "parted0")
-        cast(WB, (0, 1))
-        quantize(WB, (0, 1))
-        cast(WB, (2, 3), range(0, 1))
-        quantize(WB, (2, 3), range(0, 1))
+        cast(WB, (0, 1, 2, 3), range(0, 1), "stage_first")
+        quantize(WB, (0, 1, 2, 3), range(0, 1))
+        cast(WB, (0, 1), range(1, 2))
+        quantize(WB, (0, 1), range(1, 2))
         second_words = pick_words(1, "stage00")
 
         def bank(kind, u):
@@ -257,7 +257,10 @@ def tile_list_rgg_ownL_kernel(
         def make_gate(u, terms):
             gate_sum = bank("gate", u)
             product(gate_sum, terms, u)
-            gate[u] = ring.tile([P, HALF], F32, name="gate")
+            if u == 0:
+                gate[u] = keep.tile([P, HALF], F32, name="gate0", tag="gate0", align_bytes=64)
+            else:
+                gate[u] = ring.tile([P, HALF], F32, name="gate")
             nc.scalar.activation(gate[u][:], gate_sum[:], SIGMOID)
 
         def make_message(u):
@@ -271,12 +274,9 @@ def tile_list_rgg_ownL_kernel(
             nc.gpsimd.tensor_tensor(target[:, cols], message[u][:, cols], gate[u][:, cols], MULT)
 
         def make_own(u):
-            own_sum = bank("own", u)
+            own_sum = bank("total", 0) if u == 1 else bank("own", u)
             product(own_sum, (("wo", DST),), u)
-            if u == 1:
-                own[u] = keep.tile([P, HALF], F32, name="own1", tag="weighted0")
-            else:
-                own[u] = ring.tile([P, HALF], F32, name="own")
+            own[u] = ring.tile([P, HALF], F32, name="own")
             nc.scalar.copy(own[u][:], own_sum[:])
 
         def add_up(u, groups=range(GROUPS)):
@@ -289,9 +289,7 @@ def tile_list_rgg_ownL_kernel(
                         total[:, cols], lhsT=term[:, cols], rhs=ident[:], is_transpose=True,
                         start=(s == 0), stop=(s == len(terms) - 1),
                     )
-            if u == 0 and groups[0] == 0:
-                weighted[u, 0] = keep.tile([P, HALF], F32, name="weighted0", tag="weighted0")
-            elif u == 2:
+            if u == 2:
                 weighted[u, 0] = keep.tile([P, HALF], F32, name="weighted2", tag="raw121", align_bytes=64)
             else:
                 weighted[u, groups[0]] = ring.tile([P, HALF], F32, name="weighted")
@@ -346,14 +344,15 @@ def tile_list_rgg_ownL_kernel(
         pick_state(0, fresh(deep, "residual"))
         pick_state(1, fresh(deep, "residual"))
         cast(WB, (2, 3), range(1, 2), "stage10")
+        gated0 = keep.tile([P, HALF], F32, name="gated0", tag="stage00", align_bytes=64)[:]
         turned_weights = bank("back", 1)
         nc.tensor.transpose(turned_weights[:, 0:P], weight_rows[:], ident[:])
         edge_weight = keep.tile([P, J // P], F32, name="edge_weight")
         nc.scalar.copy(edge_weight[:], turned_weights[:, 0 : J // P])
-        pick_block_state(1)
-        gated0 = keep.tile([P, HALF], F32, name="gated0", tag="stage00", align_bytes=64)[:]
         for first in range(0, HALF, HALF // 2):
             let_through(0, gated0, slice(first, first + HALF // 2))
+        quantize(WB, (2, 3), range(1, 2), "gate0")
+        pick_block_state(1)
         last = UNITS - 1
         for step in range(1, UNITS):
             if step in ON_GPSIMD and step > 1:
@@ -378,7 +377,6 @@ def tile_list_rgg_ownL_kernel(
                 put(0, turn_back(0, range(0, 2)), 0, HALF // 2)
                 make_own(step)
                 cast(WO, (1,))
-                quantize(WB, (2, 3), range(1, 2), "raw110")
                 quantize(WO, (1,))
                 cast(WO, (2, 3))
                 quantize(WO, (2, 3))

@@ -135,6 +135,9 @@ def tile_list_rgg_ownL_kernel(
             t = keep.tile([P, len(passes), width, PACK], BF16, name=name, tag=tag or name, align_bytes=64)
             grouped[w, blocks, passes] = t
             for i, a in enumerate(passes):
+                if (w, blocks, a) == (WO, (2, 3), 0):
+                    nc.gpsimd.tensor_copy(t[:, i], raw[w, blocks[0], a][:, :, 0:width].rearrange("p i n -> p n i"))
+                    continue
                 nc.scalar.copy(
                     t[:, i].rearrange("p (c m) i -> p c i m", m=LINE),
                     raw[w, blocks[0], a][:, :, 0:width].rearrange("p i (c m) -> p c i m", m=LINE),
@@ -252,10 +255,12 @@ def tile_list_rgg_ownL_kernel(
         def result_tile(u, first=0):
             if u == 0 and first > 0:
                 return keep.tile([P, HALF], F32, name="result0", tag="raw111", align_bytes=64)
+            if u == 1:
+                return keep.tile([P, HALF], F32, name="result1", tag="stage11", align_bytes=64)
             return deep.tile([P, HALF], F32, name="result")
 
         def make_gate(u, terms):
-            gate_sum = bank("gate", u)
+            gate_sum = bank("own", 0) if u == 3 else bank("gate", u)
             product(gate_sum, terms, u)
             if u == 0:
                 gate[u] = keep.tile([P, HALF], F32, name="gate0", tag="gate0", align_bytes=64)
@@ -289,8 +294,8 @@ def tile_list_rgg_ownL_kernel(
                         total[:, cols], lhsT=term[:, cols], rhs=ident[:], is_transpose=True,
                         start=(s == 0), stop=(s == len(terms) - 1),
                     )
-            if u == 2:
-                weighted[u, 0] = keep.tile([P, HALF], F32, name="weighted2", tag="raw121", align_bytes=64)
+            if u in (2, 3):
+                weighted[u, 0] = keep.tile([P, HALF], F32, name="held", tag=("raw121", "weighted3")[u - 2], align_bytes=64)
             else:
                 weighted[u, groups[0]] = ring.tile([P, HALF], F32, name="weighted")
             for e in groups:
@@ -313,10 +318,7 @@ def tile_list_rgg_ownL_kernel(
             partial = ring.tile([P, HALF], F32, name="partial")
             first, second = (gated[u], own[u][:]) if u == 1 else (own[u][:], gated[u])
             nc.gpsimd.tensor_tensor(partial[:], first, residual[u], ADD)
-            if u == 1:
-                total = keep.tile([P, HALF], F32, name="total1", tag="stage11", align_bytes=64)
-            else:
-                total = ring.tile([P, HALF], F32, name="partial")
+            total = ring.tile([P, HALF], F32, name="partial")
             nc.gpsimd.tensor_tensor(total[:], partial[:], second, ADD)
             return total
 
@@ -369,8 +371,10 @@ def tile_list_rgg_ownL_kernel(
                 add_up(0, range(2, 4))
             elif step - 1 not in ON_GPSIMD:
                 add_up(step - 1)
-            if step in (1, 3):
-                pick_block_state(step // 2 + 2)
+            if step == 1:
+                pick_block_state(2)
+            if step == 3:
+                pick_state(5, fresh(deep, "residual"))
             if step not in ON_GPSIMD:
                 make_own(step)
             if step == 1:
@@ -382,7 +386,10 @@ def tile_list_rgg_ownL_kernel(
                 quantize(WO, (2, 3))
                 put(0, turn_back(0, range(2, 4)), HALF // 2, HALF // 2)
             elif step - 1 not in ON_GPSIMD:
-                put(step - 1, turn_back(step - 1))
+                result = turn_back(step - 1)
+                if step == 4:
+                    pick_state(7, keep.tile([P, HALF], F32, name="residual7", tag="weighted3", align_bytes=64)[:])
+                put(step - 1, result)
             if step in ON_GPSIMD and step < last:
                 put(step, weigh_on_gpsimd(step, add_on_gpsimd(step)))
         page = pages[PAGE_OF[BLOCKS - 1]]

@@ -361,8 +361,8 @@ def tile_list_rgg_ownL_kernel(
                 make_own(step)
             make_gate(step, (("wb", SRC), ("wa", DST)))
             make_message(step)
-            if step == 4:
-                tag = "stage12"
+            if step in (1, 4):
+                tag = "stage10" if step == 1 else "stage12"
                 let_through(step, keep.tile([P, HALF], F32, name="gated", tag=tag, align_bytes=64)[:])
             else:
                 let_through(step, fresh(ring, "gated"))

@@ -32,7 +32,6 @@ HALVES = J // HALF
 BLOCKS = N // P
 PAGES = 3
 SHIFT = QUAD // PASSES
-MOVED_ROWS = 112
 DST, SRC = 0, 1
 SIDES = (DST, SRC)
 UNITS = BLOCKS * HALVES
@@ -180,9 +179,8 @@ def tile_list_rgg_ownL_kernel(
         picked_scales = keep.tile([P, len(SIDES) * J], U8, name="picked_scales", align_bytes=64)
         for side in SIDES:
             nc.vector.tensor_copy(picked_scales[:, side * J : (side + 1) * J], table_scales[:].indirect(lists[side][:]))
-        nc.sync.dma_start(
-            moved_scales[0:MOVED_ROWS, :].bitcast(I32), picked_scales[SHIFT : SHIFT + MOVED_ROWS, :].bitcast(I32)
-        )
+        for r in range(ROWS):
+            nc.sync.dma_start(moved_scales[r:P:QUAD, :].bitcast(I32), picked_scales[SHIFT + r : P : QUAD, :].bitcast(I32))
         edge_scales = (picked_scales[:], moved_scales)
 
         load_floats(WO, range(0, 1), range(0, 1))

@@ -36,7 +36,7 @@ DST, SRC = 0, 1
 SIDES = (DST, SRC)
 UNITS = BLOCKS * HALVES
 GROUPS = HALF // P
-ON_GPSIMD = (1, 5, 7)
+ON_GPSIMD = (1, 6, 7)
 WB, WO = 0, 1
 ORDER = ((0, 0), (0, 1), (1, 0), (1, 1), (2, 0), (3, 0), (2, 1), (3, 1))
 PAGE_OF = (0, 1, 0, 2)
@@ -95,17 +95,15 @@ def tile_list_rgg_ownL_kernel(
 
         given_codes = {}
 
-        def load_codes(blocks):
-            sources = (
-                ("wa", wa_words.rearrange("a p c -> p a c"), 2),
-                ("wc", wc_words.rearrange("a p n i -> p a (n i)"), 4),
-            )
-            for w, words, size in sources:
-                width = size * P
-                t = keep.tile([P, PASSES, len(blocks) * width], U8, name="%s_codes%d" % (w, blocks[0]), align_bytes=64)
-                nc.sync.dma_start(t[:].bitcast(I32), words[:, :, blocks[0] * width : (blocks[-1] + 1) * width].bitcast(I32))
-                for b in blocks:
-                    given_codes[w, b] = t[:, :, (b - blocks[0]) * width : (b - blocks[0] + 1) * width]
+        def load_codes(w, blocks):
+            if w == "wa":
+                words, width = wa_words.rearrange("a p c -> p a c"), 2 * P
+            else:
+                words, width = wc_words.rearrange("a p n i -> p a (n i)"), 4 * P
+            t = keep.tile([P, PASSES, len(blocks) * width], U8, name="%s_codes%d" % (w, blocks[0]), align_bytes=64)
+            nc.sync.dma_start(t[:].bitcast(I32), words[:, :, blocks[0] * width : (blocks[-1] + 1) * width].bitcast(I32))
+            for b in blocks:
+                given_codes[w, b] = t[:, :, (b - blocks[0]) * width : (b - blocks[0] + 1) * width]
 
         parted = {}
 
@@ -170,7 +168,8 @@ def tile_list_rgg_ownL_kernel(
         nc.sync.dma_start(table_words[:], tab_words[0].rearrange("p t b -> p (t b)").bitcast(I32))
         load_scales(1, wc_scales)
         load_floats(WB, range(BLOCKS))
-        load_codes(range(0, 1))
+        load_codes("wc", range(0, 1))
+        load_codes("wa", range(BLOCKS))
         states = [keep.tile([P, T], F32, name="state%d" % b) for b in range(BLOCKS)]
 
         def load_state(b):
@@ -189,13 +188,12 @@ def tile_list_rgg_ownL_kernel(
         load_state(0)
         load_state(1)
         load_floats(WO, range(1, 2))
-        load_codes(range(1, BLOCKS))
+        load_codes("wc", range(1, BLOCKS))
         load_state(2)
-        spread_weight = [keep.tile([P, HALF], F32, name="spread_weight%d" % h) for h in range(HALVES)]
-        nc.sync.dma_start(spread_weight[1][:], wgo[:, HALF:J])
+        spread_weight = keep.tile([P, HALF], F32, name="spread_weight")
+        nc.sync.dma_start(spread_weight[:], wgo[:, HALF:J])
         load_floats(WO, range(2, BLOCKS))
         load_state(3)
-        nc.sync.dma_start(spread_weight[0][:], wgo[:, 0:HALF])
 
         part_words(pick_words(0, "both0"), 0, "parted0")
         cast(WB, (0, 1, 2, 3), range(0, 1), "stage_first")
@@ -322,7 +320,7 @@ def tile_list_rgg_ownL_kernel(
 
         def weigh_on_gpsimd(u, total):
             result = result_tile(u)
-            nc.gpsimd.tensor_tensor(result[:], total[:], spread_weight[ORDER[u][1]][:], MULT)
+            nc.gpsimd.tensor_tensor(result[:], total[:], spread_weight[:], MULT)
             return result
 
         def put(u, result, first=0, count=HALF):
@@ -391,5 +389,5 @@ def tile_list_rgg_ownL_kernel(
             if step in ON_GPSIMD and step < last:
                 put(step, weigh_on_gpsimd(step, add_on_gpsimd(step)))
         page = pages[PAGE_OF[BLOCKS - 1]]
-        nc.vector.tensor_tensor(page[:].indirect(offsets(DST, HALF, HALF)), add_on_gpsimd(last)[:], spread_weight[1][:], MULT)
+        nc.vector.tensor_tensor(page[:].indirect(offsets(DST, HALF, HALF)), add_on_gpsimd(last)[:], spread_weight[:], MULT)
         nc.sync.dma_start(out[(BLOCKS - 1) * P : BLOCKS * P, :], page[:])

@@ -61,7 +61,9 @@ def tile_list_rgg_ownL_kernel(
             return lists[side][:, first // STRIPE : (first + count) // STRIPE]
 
         table_scales = keep.tile([P, T], U8, name="table_scales", align_bytes=64)
-        nc.gpsimd.memset(table_scales[:].bitcast(I32), 0)
+        scale_words = table_scales[:].bitcast(I32)
+        nc.vector.memset(scale_words[:, 0 : T // 8 - 1], 0)
+        nc.vector.memset(scale_words[:, T // 8 - 1 :], 0)
         warm = keep.tile([P, 2], F32, name="warm")
         nc.gpsimd.memset(warm[:, 0:1], 0.0)
         planes = keep.tile([P, 2 * PASSES * N + len(SIDES) * J], U8, name="planes", align_bytes=64)

from contextlib import ExitStack

import concourse.mybir as mybir
from concourse.masks import make_identity

K, N, T, J = 1024, 512, 2048, 1024
FLOPS = 2 * 4 * K * N * J

F32 = mybir.dt.float32
BF16 = mybir.dt.bfloat16
I32 = mybir.dt.int32
U32 = mybir.dt.uint32
U16 = mybir.dt.uint16
U8 = mybir.dt.uint8
FP8X4 = mybir.dt.float8_e4m3fn_x4
FP4X4 = mybir.dt.float4_e2m1fn_x4
MULT = mybir.AluOpType.mult
COPY = mybir.ActivationFunctionType.Copy
ADD = mybir.AluOpType.add
SIGMOID = mybir.ActivationFunctionType.Sigmoid

P = 128
PACK = 4
PASSES = K // (P * PACK)
QUADS = 4
QUAD = P // QUADS
ROWS = 4
STRIPE = 16
LINE = 4
HALF = 512
HALVES = J // HALF
BLOCKS = N // P
PAGES = 3
SHIFT = QUAD // PASSES
DST, SRC = 0, 1
SIDES = (DST, SRC)
UNITS = BLOCKS * HALVES
GROUPS = HALF // P
ON_GPSIMD = (1, 6, 7)
WB, WO = 0, 1
ORDER = ((0, 0), (0, 1), (1, 0), (1, 1), (2, 0), (3, 0), (2, 1), (3, 1))
PAGE_OF = (0, 1, 0, 2)
BANKS = {"gate": 2, "message": 1, "own": 1, "total": 2, "back": 2}


def tile_list_rgg_ownL_kernel(
    tc, tab_words, tab_scales, wa_words, wa_scales, wb, wc_words, wc_scales, wo, rT, wgo, offs, offs2, out
):
    nc = tc.nc
    with ExitStack() as ctx:
        keep = ctx.enter_context(tc.tile_pool(name="keep", bufs=1))
        ring = ctx.enter_context(tc.tile_pool(name="ring", bufs=2))
        deep = ctx.enter_context(tc.tile_pool(name="deep", bufs=4))
        psum = ctx.enter_context(tc.psum_pool(name="psum", bufs=1))

        dst_list = keep.tile([P, J // STRIPE], U16, name="dst_list")
        src_list = keep.tile([P, J // STRIPE], U16, name="src_list")
        lists = (dst_list, src_list)

        def offsets(side, first, count):
            return lists[side][:, first // STRIPE : (first + count) // STRIPE]

        table_scales = keep.tile([P, T], U8, name="table_scales", align_bytes=64)
        scale_words = table_scales[:].bitcast(I32)
        nc.vector.memset(scale_words[:, 0 : T // 8 - 1], 0)
        nc.vector.memset(scale_words[:, T // 8 - 1 :], 0)
        warm = keep.tile([P, 2], F32, name="warm")
        nc.gpsimd.memset(warm[:, 0:1], 0.0)
        planes = keep.tile([P, 2 * PASSES * N + len(SIDES) * J], U8, name="planes", align_bytes=64)
        nc.gpsimd.memset(planes[:].bitcast(I32), 0)
        given_scales = planes[:, 0 : 2 * PASSES * N].rearrange("p (w a n) -> p w a n", w=2, a=PASSES)
        moved_scales = planes[:, 2 * PASSES * N :]
        ident = keep.tile([P, P], F32, name="ident")
        make_identity(nc, ident[:])
        pages = [keep.tile([P, T], F32, name="page%d" % i) for i in range(PAGES)]
        for page in pages:
            nc.gpsimd.memset(page[:].bitcast(I32), 0)

        float_weights = (wb, wo)
        raw = {}

        def load_floats(w, blocks, passes=range(PASSES)):
            for a in passes:
                name = "raw%d%d%d" % (w, blocks[0], a)
                t = keep.tile([P, PACK, len(blocks) * P], F32, name=name, tag=name, align_bytes=64)
                rows = float_weights[w][a * P * PACK : (a + 1) * P * PACK, blocks[0] * P : (blocks[-1] + 1) * P]
                nc.sync.dma_start(t[:], rows.rearrange("(p i) n -> p i n", i=PACK))
                for b in blocks:
                    raw[w, b, a] = t[:, :, (b - blocks[0]) * P :]

        def load_scales(w, scales):
            for q in range(QUADS):
                nc.sync.dma_start(
                    given_scales[QUAD * q : QUAD * q + ROWS, w, :, :].bitcast(I32),
                    scales[:, ROWS * q : ROWS * (q + 1), :].rearrange("a r n -> r a n").bitcast(I32),
                )

        given_codes = {}

        def load_codes(w, blocks):
            if w == "wa":
                words, width = wa_words.rearrange("a p c -> p a c"), 2 * P
            else:
                words, width = wc_words.rearrange("a p n i -> p a (n i)"), 4 * P
            t = keep.tile([P, PASSES, len(blocks) * width], U8, name="%s_codes%d" % (w, blocks[0]), align_bytes=64)
            nc.sync.dma_start(t[:].bitcast(I32), words[:, :, blocks[0] * width : (blocks[-1] + 1) * width].bitcast(I32))
            for b in blocks:
                given_codes[w, b] = t[:, :, (b - blocks[0]) * width : (b - blocks[0] + 1) * width]

        parted = {}

        def pick_words(h, tag):
            both = keep.tile([P, len(SIDES) * HALF], I32, name="both%d" % h, tag=tag, align_bytes=64)
            for side in (SRC, DST):
                window = table_words[:].bitcast(U32)
                nc.vector.tensor_copy(
                    both[:, side * HALF : (side + 1) * HALF].bitcast(U32), window.indirect(offsets(side, h * HALF, HALF))
                )
            return both

        def part_words(both, h, tag):
            t = keep.tile([P, len(SIDES), PASSES, 2 * HALF], U8, name="parted%d" % h, tag=tag, align_bytes=64)
            for side in (SRC, DST):
                pairs = both[:, side * HALF : (side + 1) * HALF].bitcast(U16)
                nc.vector.tensor_copy(t[:, side].bitcast(U16), pairs.rearrange("p (j a) -> p a j", a=PASSES))
                parted[side, h] = t[:, side]

        grouped = {}
        made = {}

        def cast(w, blocks, passes=range(PASSES), tag=""):
            name = "stage%d%d" % (w, blocks[0])
            width = len(blocks) * P
            t = keep.tile([P, len(passes), width, PACK], BF16, name=name, tag=tag or name, align_bytes=64)
            grouped[w, blocks, passes] = t
            for i, a in enumerate(passes):
                if (w, blocks, a) == (WO, (2, 3), 0):
                    nc.gpsimd.tensor_copy(t[:, i], raw[w, blocks[0], a][:, :, 0:width].rearrange("p i n -> p n i"))
                    continue
                nc.scalar.copy(
                    t[:, i].rearrange("p (c m) i -> p c i m", m=LINE),
                    raw[w, blocks[0], a][:, :, 0:width].rearrange("p i (c m) -> p c i m", m=LINE),
                )

        def quantize(w, blocks, passes=range(PASSES), tag=""):
            shape = [P, len(passes), len(blocks) * P]
            name = "%d%d%d" % (w, blocks[0], passes[0])
            codes = keep.tile(shape, U32, name="codes" + name, tag=tag or "codes" + name, align_bytes=64)
            scales = keep.tile(shape, U8, name="scales" + name, align_bytes=64)
            nc.vector.quantize_mx(
                out=codes[:].rearrange("p a n -> p (a n)").bitcast(FP8X4),
                scales=scales[:].rearrange("p a n -> p (a n)"),
                in_=grouped[w, blocks, passes][:].rearrange("p a n i -> p (a n i)"),
            )
            for i, b in enumerate(blocks):
                for n, a in enumerate(passes):
                    made[w, b, a] = (codes[:, n, i * P : (i + 1) * P], scales[:, n, i * P : (i + 1) * P])

        nc.sync.dma_start(dst_list[:], offs2)
        weight_rows = keep.tile([P, P], F32, name="weight_rows")
        nc.sync.dma_start(weight_rows[:], wgo[0 : P * P // J, :].rearrange("r (e p) -> (r e) p", p=P))
        nc.sync.dma_start(src_list[:], offs)
        for r in range(ROWS):
            nc.sync.dma_start(
                table_scales[r : P : SHIFT, :].bitcast(I32),
                tab_scales.rearrange("a (q r) t -> r q a t", r=ROWS)[r].bitcast(I32),
            )
        nc.scalar.activation(warm[:, 1:2], warm[:, 0:1], SIGMOID)
        table_words = keep.tile([P, T], I32, name="table_words", align_bytes=64)
        nc.sync.dma_start(table_words[:], tab_words[0].rearrange("p t b -> p (t b)").bitcast(I32))
        load_scales(1, wc_scales)
        load_floats(WB, range(BLOCKS))
        load_codes("wc", range(0, 1))
        load_codes("wa", range(BLOCKS))
        states = [keep.tile([P, T], F32, name="state%d" % b) for b in range(BLOCKS)]

        def load_state(b):
            nc.sync.dma_start(states[b][:], rT[b * P : (b + 1) * P, :])

        picked_scales = keep.tile([P, len(SIDES) * J], U8, name="picked_scales", align_bytes=64)
        for side in SIDES:
            nc.vector.tensor_copy(picked_scales[:, side * J : (side + 1) * J], table_scales[:].indirect(lists[side][:]))
        for r in range(ROWS):
            nc.sync.dma_start(moved_scales[r:P:QUAD, :].bitcast(I32), picked_scales[SHIFT + r : P : QUAD, :].bitcast(I32))
        edge_scales = (picked_scales[:], moved_scales)

        load_floats(WO, range(0, 1), range(0, 1))
        load_scales(0, wa_scales)
        load_floats(WO, range(0, 1), range(1, 2))
        load_state(0)
        load_state(1)
        load_floats(WO, range(1, 2))
        load_codes("wc", range(1, BLOCKS))
        load_state(2)
        spread_weight = keep.tile([P, HALF], F32, name="spread_weight")
        nc.sync.dma_start(spread_weight[:], wgo[:, HALF:J])
        load_floats(WO, range(2, BLOCKS))
        load_state(3)

        part_words(pick_words(0, "both0"), 0, "parted0")
        cast(WB, (0, 1, 2, 3), range(0, 1), "stage_first")
        quantize(WB, (0, 1, 2, 3), range(0, 1))
        cast(WB, (0, 1), range(1, 2))
        quantize(WB, (0, 1), range(1, 2))
        second_words = pick_words(1, "stage00")

        def bank(kind, u):
            return psum.tile([P, HALF], F32, name="bank", tag="%s%d" % (kind, u % BANKS[kind]))

        def weight(w, a, b):
            cols = slice(b * P, (b + 1) * P)
            if w == "wa":
                return given_codes[w, b][:, a, :].bitcast(FP4X4), given_scales[:, 0, a, cols]
            if w == "wc":
                return given_codes[w, b][:, a, :].bitcast(FP8X4), given_scales[:, 1, a, cols]
            codes, scales = made[("wb", "wo").index(w), b, a]
            return codes.bitcast(FP8X4), scales

        def product(acc, terms, u):
            b, h = ORDER[u]
            steps = [(w, side, a) for w, side in terms for a in reversed(range(PASSES))]
            for s, (w, side, a) in enumerate(steps):
                codes, scales = weight(w, a, b)
                column = side * J + h * HALF
                nc.tensor.matmul_mx(
                    out=acc[:],
                    lhsT=codes,
                    lhsT_scale=scales,
                    rhs=parted[side, h][:, a, :].bitcast(FP4X4),
                    rhs_scale=edge_scales[a][:, column : column + HALF],
                    start=(s == 0),
                    stop=(s == len(steps) - 1),
                )

        residual = {}
        gate = {}
        message = {}
        gated = {}
        own = {}
        weighted = {}

        def pick_state(u, target):
            b, h = ORDER[u]
            residual[u] = target
            nc.vector.tensor_copy(target, states[b][:].indirect(offsets(DST, h * HALF, HALF)))

        def pick_block_state(b):
            whole = keep.tile([P, J], F32, name="residual_block%d" % b)
            nc.vector.tensor_copy(whole[:], states[b][:].indirect(dst_list[:]))
            for h in range(HALVES):
                residual[ORDER.index((b, h))] = whole[:, h * HALF : (h + 1) * HALF]

        def result_tile(u, first=0):
            if u == 0 and first > 0:
                return keep.tile([P, HALF], F32, name="result0", tag="raw111", align_bytes=64)
            if u == 1:
                return keep.tile([P, HALF], F32, name="result1", tag="stage11", align_bytes=64)
            return deep.tile([P, HALF], F32, name="result")

        def make_gate(u, terms):
            gate_sum = bank("own", 0) if u == 3 else bank("gate", u)
            product(gate_sum, terms, u)
            if u == 0:
                gate[u] = keep.tile([P, HALF], F32, name="gate0", tag="gate0", align_bytes=64)
            else:
                gate[u] = ring.tile([P, HALF], F32, name="gate")
            nc.scalar.activation(gate[u][:], gate_sum[:], SIGMOID)

        def make_message(u):
            message_sum = bank("message", u)
            product(message_sum, (("wc", SRC),), u)
            message[u] = ring.tile([P, HALF], F32, name="message")
            nc.scalar.copy(message[u][:], message_sum[:])

        def let_through(u, target, cols=slice(0, HALF)):
            gated[u] = target
            nc.gpsimd.tensor_tensor(target[:, cols], message[u][:, cols], gate[u][:, cols], MULT)

        def make_own(u):
            own_sum = bank("total", 0) if u == 1 else bank("own", u)
            product(own_sum, (("wo", DST),), u)
            own[u] = ring.tile([P, HALF], F32, name="own")
            nc.scalar.copy(own[u][:], own_sum[:])

        def add_up(u, groups=range(GROUPS)):
            total = bank("total", u + groups[0] // 2)
            terms = (gated[u], own[u][:], residual[u])
            for e in groups:
                cols = slice(e * P, (e + 1) * P)
                for s, term in enumerate(terms):
                    nc.tensor.matmul(
                        total[:, cols], lhsT=term[:, cols], rhs=ident[:], is_transpose=True,
                        start=(s == 0), stop=(s == len(terms) - 1),
                    )
            if u in (2, 3):
                weighted[u, 0] = keep.tile([P, HALF], F32, name="held", tag=("raw121", "weighted3")[u - 2], align_bytes=64)
            else:
                weighted[u, groups[0]] = ring.tile([P, HALF], F32, name="weighted")
            for e in groups:
                cols = slice(e * P, (e + 1) * P)
                g = ORDER[u][1] * GROUPS + e
                scale = edge_weight[:, g : g + 1]
                nc.scalar.activation(weighted[u, groups[0]][:, cols], total[:, cols], COPY, scale=scale)

        def turn_back(u, groups=range(GROUPS)):
            back = bank("back", u + groups[0] // 2)
            for e in groups:
                cols = slice(e * P, (e + 1) * P)
                nc.tensor.transpose(back[:, cols], weighted[u, groups[0]][:, cols], ident[:])
            result = result_tile(u, groups[0])
            cols = slice(groups[0] * P, (groups[-1] + 1) * P)
            nc.scalar.copy(result[:, cols], back[:, cols])
            return result

        def add_on_gpsimd(u):
            partial = ring.tile([P, HALF], F32, name="partial")
            first, second = (gated[u], own[u][:]) if u == 1 else (own[u][:], gated[u])
            nc.gpsimd.tensor_tensor(partial[:], first, residual[u], ADD)
            total = ring.tile([P, HALF], F32, name="partial")
            nc.gpsimd.tensor_tensor(total[:], partial[:], second, ADD)
            return total

        def weigh_on_gpsimd(u, total):
            result = result_tile(u)
            nc.gpsimd.tensor_tensor(result[:], total[:], spread_weight[:], MULT)
            return result

        def put(u, result, first=0, count=HALF):
            b, h = ORDER[u]
            page = pages[PAGE_OF[b]]
            nc.vector.tensor_copy(page[:].indirect(offsets(DST, h * HALF + first, count)), result[:, first : first + count])
            if h == HALVES - 1:
                nc.sync.dma_start(out[b * P : (b + 1) * P, :], page[:])

        def fresh(pool, name):
            return pool.tile([P, HALF], F32, name=name)[:]

        make_message(0)
        make_gate(0, (("wb", SRC), ("wa", DST)))
        cast(WO, (0,))
        quantize(WO, (0,))
        make_own(0)
        part_words(second_words, 1, "raw101")
        pick_state(0, fresh(deep, "residual"))
        pick_state(1, fresh(deep, "residual"))
        cast(WB, (2, 3), range(1, 2), "stage10")
        gated0 = keep.tile([P, HALF], F32, name="gated0", tag="stage00", align_bytes=64)[:]
        turned_weights = bank("back", 1)
        nc.tensor.transpose(turned_weights[:, 0:P], weight_rows[:], ident[:])
        edge_weight = keep.tile([P, J // P], F32, name="edge_weight")
        nc.scalar.copy(edge_weight[:], turned_weights[:, 0 : J // P])
        for first in range(0, HALF, HALF // 2):
            let_through(0, gated0, slice(first, first + HALF // 2))
        quantize(WB, (2, 3), range(1, 2), "gate0")
        pick_block_state(1)
        last = UNITS - 1
        for step in range(1, UNITS):
            if step in ON_GPSIMD and step > 1:
                make_own(step)
            make_gate(step, (("wb", SRC), ("wa", DST)))
            make_message(step)
            if step in (1, 4):
                tag = "stage10" if step == 1 else "stage12"
                let_through(step, keep.tile([P, HALF], F32, name="gated", tag=tag, align_bytes=64)[:])
            else:
                let_through(step, fresh(ring, "gated"))
            if step == 1:
                add_up(0, range(0, 2))
                add_up(0, range(2, 4))
            elif step - 1 not in ON_GPSIMD:
                add_up(step - 1)
            if step == 1:
                pick_block_state(2)
            if step == 3:
                pick_state(5, fresh(deep, "residual"))
            if step not in ON_GPSIMD:
                make_own(step)
            if step == 1:
                put(0, turn_back(0, range(0, 2)), 0, HALF // 2)
                make_own(step)
                cast(WO, (1,))
                quantize(WO, (1,))
                cast(WO, (2, 3))
                quantize(WO, (2, 3))
                put(0, turn_back(0, range(2, 4)), HALF // 2, HALF // 2)
            elif step - 1 not in ON_GPSIMD:
                result = turn_back(step - 1)
                if step == 4:
                    pick_state(7, keep.tile([P, HALF], F32, name="residual7", tag="weighted3", align_bytes=64)[:])
                put(step - 1, result)
            if step in ON_GPSIMD and step < last:
                put(step, weigh_on_gpsimd(step, add_on_gpsimd(step)))
        page = pages[PAGE_OF[BLOCKS - 1]]
        nc.vector.tensor_tensor(page[:].indirect(offsets(DST, HALF, HALF)), add_on_gpsimd(last)[:], spread_weight[:], MULT)
        nc.sync.dma_start(out[(BLOCKS - 1) * P : BLOCKS * P, :], page[:])
